import numpy as np, ml_dtypes
CORES = [5,29,101,125,133,157,229,253]
N = 8
R, W, T = 4096, 256, 512
CAPP = 128
def entries(a): return a.T.reshape(-1)
def pack(v, P): return np.ascontiguousarray(np.asarray(v, np.int32).reshape(-1, P).T)
def lists(rng, how):
    I = rng.integers(0, N * R, (N, T))
    O = np.stack([rng.permutation(np.repeat(np.arange(N), CAPP))[:T] for r in range(N)])
    if how == "full": O = np.stack([rng.permutation(np.repeat(rng.permutation(N)[:T // CAPP], CAPP)) for r in range(N)])
    I = R * O + rng.integers(0, R, (N, T))
    if how == "alike": I = R * O + rng.integers(0, R, (N, 1))
    if how == "edge": I = R * O + np.where(rng.random((N, T)) < 0.5, 0, R - 1)
    if how == "sorted": I = np.sort(I, axis=1)
    return {"idx": np.stack([pack(I[r], 128) for r in range(N)])}
def setup_inputs(rng):
    return dict({"tab": rng.standard_normal((N, R, W), dtype=np.float32).astype(ml_dtypes.bfloat16)}, **lists(rng, "uniform"))
def setup_inputs_alike(rng):
    d = setup_inputs(rng); d.update(lists(rng, "alike"))
    for k in ("tab",): d[k] = (d[k].astype(np.float32) * 1048576.0).astype(d[k].dtype)
    return d
def setup_inputs_edge(rng):
    d = setup_inputs(rng); d.update(lists(rng, "edge"))
    for k in ("tab",): d[k] = (d[k].astype(np.float32) * (1 / 1024.0)).astype(d[k].dtype)
    return d
def setup_inputs_full(rng):
    d = setup_inputs(rng); d.update(lists(rng, "full"))
    return d
def setup_inputs_sorted(rng):
    d = setup_inputs(rng); d.update(lists(rng, "sorted"))
    return d
def check_inputs(x):
    bad = []
    if x["idx"].min() < 0 or x["idx"].max() >= N * R: bad.append("idx out of range")
    if max(int(np.bincount(entries(a) // R, minlength=N).max()) for a in x["idx"]) > CAPP: bad.append("more than CAPP entries of a list point into one rank's part")
    return bad
def reference(tab, idx):
    A = np.concatenate(list(tab), axis=0)
    return {"y": np.stack([A[entries(idx[r])] for r in range(N)])}

@@ -1,0 +1,312 @@
+import numpy as np
+from concourse.bass import DstId, RemoteDMATransfer
+from concourse.bass import IndirectOffsetOnAxis
+from concourse.mybir import AluOpType, AxisListType, ActivationFunctionType
+
+NSIM = 256
+N = 8
+W = 256
+CAP = 128
+NPOOL = 64
+
+SCRATCH = {
+    "ix": ("sbuf", [128, 4], "int32"),
+    "owi": ("sbuf", [128, 4], "int32"),
+    "lci": ("sbuf", [128, 8], "int32"),
+    "owf": ("sbuf", [128, 4], "float32"),
+    "lcf": ("sbuf", [128, 8], "float32"),
+    "io8": ("sbuf", [128, 8], "float32"),
+    "ohz": ("sbuf", [128, 56], "bfloat16"),
+    "ones": ("sbuf", [128, 128], "bfloat16"),
+    "upper": ("sbuf", [128, 128], "bfloat16"),
+    "ident": ("sbuf", [128, 128], "bfloat16"),
+    "io128": ("sbuf", [128, 128], "bfloat16"),
+    "rv": ("sbuf", [128, 64], "bfloat16"),
+    "prod": ("sbuf", [128, 32], "float32"),
+    "pos": ("sbuf", [128, 4], "float32"),
+    "pm": ("sbuf", [128, 512], "bfloat16"),
+    "la": ("sbuf", [128, 8], "float32"),
+    "req": ("sbuf", [128, 8], "int32"),
+    "reqland": ("sbuf", [128, 64], "int32"),
+    "ow256": ("sbuf", [128, 4], "float32"),
+    "slot": ("sbuf", [128, 4], "float32"),
+    "pidx": ("sbuf", [128, 1], "int32"),
+    "pci": ("sbuf", [128, 3], "int32"),
+    "pcf": ("sbuf", [128, 3], "float32"),
+    "kcol": ("sbuf", [128, 1], "float32"),
+    "rowm": ("sbuf", [128, 128], "float32"),
+    "vmask": ("sbuf", [128, 128], "float32"),
+    "emat": ("sbuf", [128, 128], "float32"),
+    "mmat": ("sbuf", [128, 128], "float32"),
+    "orh": ("sbuf", [128, 128], "float32"),
+    "off": ("sbuf", [128, 32], "uint16"),
+    "gat": ("sbuf", [128, N * W], "bfloat16"),
+    "land": ("sbuf", [128, N * W], "bfloat16"),
+    "rtw": ("sbuf", [128, N * W], "bfloat16"),
+    "yt": ("sbuf", [128, 1024], "bfloat16"),
+    "ysb": ("sbuf", [128, 1024], "bfloat16"),
+    "rl": ("sbuf", [128, 8], "int32"),
+    "rt": ("sbuf", [128, 2 * W], "bfloat16"),
+    "pc": ("psum", [128, 512], "float32"),
+    "pl": ("psum", [128, 512], "float32"),
+    "po": ("psum", [128, 512], "float32"),
+    "pin0": ("psum", [128, 1024], "bfloat16"),
+    "pin1": ("psum", [128, 1024], "bfloat16"),
+    "pout0": ("psum", [128, 1024], "bfloat16"),
+    "pout1": ("psum", [128, 1024], "bfloat16"),
+}
+SEMAPHORES = (["c%d" % k for k in range(NPOOL)] + ["rs%d" % k for k in range(N)] + ["ar%d" % k for k in range(N)]
+              + ["gs%d" % k for k in range(N)] + ["rq", "rt0", "rt1", "ls"])
+
+
+def _bits(mask):
+    return [b for b in range(16) if (mask >> b) & 1]
+
+
+def _mk(bl):
+    return int(sum(1 << b for b in bl))
+
+
+def _plan(topo, cores, r):
+    me = cores[r]
+    same = sorted([q for q in range(len(cores)) if q != r and topo.may_write(me, cores[q])], key=lambda q: q ^ r)
+    cross = sorted([q for q in range(len(cores)) if q != r and q not in same], key=lambda q: q ^ r)
+    mates = [c for c in range(NSIM) if c != me and topo.host(c) == topo.host(me) and topo.chip(c) == topo.chip(me)]
+    relays = [c for c in mates if topo.die(c) == topo.die(me) and all(topo.may_write(c, cores[q]) for q in cross)][:2]
+    return same, cross, relays
+
+
+def _split_direct(lo):
+    h, q = len(lo) // 2, len(lo) // 4
+    return [lo[0:h], lo[h:h + q], lo[h + q:h + 2 * q]]
+
+
+def _relay(g, core, T, topo, cores, r, cross, i):
+    peers = cross[i::2]
+    lo = _bits(topo.mask(core, cores[peers[0]]))
+    half = len(lo) // 2
+    hi_n = (len(_bits(topo.mask(cores[r], core))) - len(lo)) // 2
+    g.wait_ge(T.sem.rq, hi_n)
+    trs = []
+    for j, q in enumerate(peers):
+        rid, pid = topo.addr(cores[q], core)
+        trs.append(RemoteDMATransfer(dst_ids=[DstId(rid=rid, pnc=pid)], dma_engine_mask=_mk(lo[half * j:half * j + half]),
+                                     remote_sem=T.sem["rs%d" % r], src=T.rl[:, :], dst=T.reqland[:, 8 * r:8 * r + 8]))
+    g.remote_dma_fused(trs, local_sem=T.sem.ls)
+    for j, q in enumerate(peers):
+        rid, pid = topo.addr(cores[q], core)
+        g.wait_ge(T.sem["rt%d" % j], 2 * hi_n)
+        g.remote_dma(out_ap=T.land[:, W * r:W * r + W], in_ap=T.rt[:, W * j:W * j + W], remote_sem=T.sem["ar%d" % r],
+                     local_sem=T.sem.ls, pid=pid, routing_id=rid, dma_engine_mask=_mk(lo))
+    g.wait_ge(T.sem.ls, 2 * half + 2 * len(lo))
+
+
+def rank_program(g, core, T, topo):
+    cores = [int(c) for c in T.cores]
+    r = T.rank_of(core)
+    if r is None:
+        for q, rc in enumerate(cores):
+            if topo.host(rc) == topo.host(core) and topo.chip(rc) == topo.chip(core):
+                same, cross, relays = _plan(topo, cores, q)
+                if core in relays:
+                    _relay(g, core, T, topo, cores, q, cross, relays.index(core))
+        return
+
+    V, TE, SC, SY = g.vector, g.tensor, g.scalar, g.sync
+    A = AluOpType
+    cnt = [0]
+
+    def sem():
+        cnt[0] += 1
+        return T.sem["c%d" % (cnt[0] - 1)]
+
+    same, cross, relays = _plan(topo, cores, r)
+    lo = _bits(topo.mask(core, cores[same[0]]))
+    hi = [b for b in _bits(topo.mask(core, relays[0])) if b not in lo]
+    hh = len(hi) // 2
+
+    s_ix, s_ones, s_z = sem(), sem(), sem()
+    SY.dma_start(T.ix[:, :], T.idx[:, :]).then_inc(s_ix, 16)
+    V.memset(T.ones[:, :], 1.0).then_inc(s_ones, 1)
+    V.memset(T.ohz[:, 0:24], 0.0).then_inc(s_z, 1)
+    s_io8, s_up, s_io128, s_id, s_pidx, s_rowm, s_vm = sem(), sem(), sem(), sem(), sem(), sem(), sem()
+    g.iota(T.io8[:, :], [[1, 8]], 0, 0, allow_small_or_imprecise_dtypes=True).then_inc(s_io8, 1)
+    g.wait_ge(s_ones, 1)
+    g.affine_select(T.upper[:, :], T.ones[:, :], [[1, 128]], A.is_ge, 0.0, -1, -1).then_inc(s_up, 1)
+    g.iota(T.io128[:, :], [[1, 128]], 0, 0, allow_small_or_imprecise_dtypes=True).then_inc(s_io128, 1)
+    g.affine_select(T.ident[:, :], T.ones[:, :], [[-1, 128]], A.is_equal, 0.0, 0, 1).then_inc(s_id, 1)
+    g.iota(T.pidx[:, :], [[1, 1]], 0, 1).then_inc(s_pidx, 1)
+    g.iota(T.rowm[:, :], [[0, 8], [1, 16]], 0, 0, allow_small_or_imprecise_dtypes=True).then_inc(s_rowm, 1)
+    g.iota(T.vmask[:, :], [[-16, 2], [-4, 2], [1, 32]], 0, 0, allow_small_or_imprecise_dtypes=True).then_inc(s_vm, 1)
+
+    a1, a2, a3, a4, a5, a6, a7, a8 = sem(), sem(), sem(), sem(), sem(), sem(), sem(), sem()
+    b1, b2, a10, a11 = sem(), sem(), sem(), sem()
+    a9 = [sem() for c in range(4)]
+    V.wait_ge(s_ix, 16)
+    V.tensor_scalar(T.owi[:, :], T.ix[:, :], 12, None, A.logical_shift_right).then_inc(a1, 1)
+    V.tensor_scalar(T.lci[:, 0:4], T.ix[:, :], 4032, None, A.bitwise_and).then_inc(a3, 1)
+    V.tensor_scalar(T.lci[:, 4:8], T.ix[:, :], 63, None, A.bitwise_and).then_inc(a3, 1)
+    V.wait_ge(a1, 1)
+    V.tensor_copy(T.owf[:, :], T.owi[:, :]).then_inc(a2, 1)
+    V.wait_ge(a2, 1)
+    V.wait_ge(s_io8, 1)
+    for c in range(4):
+        V.tensor_scalar(T.ohz[:, 24 + 8 * c:32 + 8 * c], T.io8[:, :], T.owf[:, c:c + 1], None, A.is_equal).then_inc(a4, 1)
+    V.wait_ge(a3, 2)
+    V.tensor_copy(T.lcf[:, :], T.lci[:, :]).then_inc(a5, 1)
+
+    TE.wait_ge(a4, 4)
+    TE.wait_ge(s_z, 1)
+    TE.wait_ge(s_up, 1)
+    TE.wait_ge(s_ones, 1)
+    TE.matmul(T.pc[:, 0:32], T.upper[:, :], T.ohz[:, 24:56], True, False).then_inc(b1, 1)
+    for k in range(1, 4):
+        TE.matmul(T.pc[:, 0:32], T.ones[:, :], T.ohz[:, 24 - 8 * k:56 - 8 * k], False, k == 3).then_inc(b1, 1)
+
+    SC.wait_ge(a4, 4)
+    SC.wait_ge(a5, 1)
+    for c in range(4):
+        for part in range(2):
+            SC.activation(T.rv[:, 16 * c + 8 * part:16 * c + 8 * part + 8], T.ohz[:, 24 + 8 * c:32 + 8 * c],
+                          ActivationFunctionType.Copy, scale=T.lcf[:, 4 * part + c:4 * part + c + 1]).then_inc(a6, 1)
+
+    V.wait_ge(b1, 4)
+    V.tensor_tensor(T.prod[:, :], T.ohz[:, 24:56], T.pc[:, 0:32], A.mult).then_inc(a7, 1)
+    V.wait_ge(a7, 1)
+    for c in range(4):
+        V.tensor_reduce(T.pos[:, c:c + 1], T.prod[:, 8 * c:8 * c + 8], AxisListType.X, A.add).then_inc(a8, 1)
+    V.wait_ge(a8, 4)
+    V.wait_ge(s_io128, 1)
+    for c in range(4):
+        V.tensor_scalar(T.pm[:, 128 * c:128 * c + 128], T.io128[:, :], T.pos[:, c:c + 1], None, A.is_equal).then_inc(a9[c], 1)
+    TE.wait_ge(a6, 8)
+    for c in range(4):
+        TE.wait_ge(a9[c], 1)
+        TE.matmul(T.pl[:, 0:16], T.pm[:, 128 * c:128 * c + 128], T.rv[:, 16 * c:16 * c + 16], c == 0, c == 3).then_inc(b2, 1)
+    V.wait_ge(b2, 4)
+    V.tensor_copy(T.la[:, :], T.pl[:, 0:8]).then_inc(a10, 1)
+    V.wait_ge(a10, 1)
+    V.tensor_tensor(T.req[:, :], T.la[:, :], T.pl[:, 8:16], A.add).then_inc(a11, 1)
+
+    g.wait_ge(a11, 1)
+    trs = []
+    for q, bl in zip(same, _split_direct(lo)):
+        rid, pid = topo.addr(cores[q], core)
+        trs.append(RemoteDMATransfer(dst_ids=[DstId(rid=rid, pnc=pid)], dma_engine_mask=_mk(bl),
+                                     remote_sem=T.sem["rs%d" % r], src=T.req[:, :], dst=T.reqland[:, 8 * r:8 * r + 8]))
+    for i, c in enumerate(relays):
+        rid, pid = topo.addr(c, core)
+        trs.append(RemoteDMATransfer(dst_ids=[DstId(rid=rid, pnc=pid)], dma_engine_mask=_mk(hi[hh * i:hh * i + hh]),
+                                     remote_sem=T.sem.rq, src=T.req[:, :], dst=T.rl[:, :]))
+    g.remote_dma_fused(trs, local_sem=T.sem.ls)
+    sent = [sum(len(bl) for bl in _split_direct(lo)) + 2 * hh]
+
+    def req_count(q):
+        qs, qc, qr = _plan(topo, cores, q)
+        if r in qs:
+            return len(_split_direct(_bits(topo.mask(cores[q], core)))[qs.index(r)])
+        return len(_bits(topo.mask(qr[0], core))) // 2
+
+    def gather(q):
+        if q == r:
+            tile, out = T.req[:, r:r + 1], T.land[:, W * r:W * r + W]
+        else:
+            g.wait_ge(T.sem["rs%d" % q], req_count(q))
+            tile, out = T.reqland[:, 8 * q + r:8 * q + r + 1], T.gat[:, W * q:W * q + W]
+        g.indirect_dma_start(out=out, out_offset=None, in_=T.tab[:], in_offset=IndirectOffsetOnAxis(ap=tile, axis=0),
+                             bounds_check=4095).then_inc(T.sem["gs%d" % q], 16)
+
+    def send(q):
+        g.wait_ge(T.sem["gs%d" % q], 16)
+        if q in same:
+            rid, pid = topo.addr(cores[q], core)
+            g.remote_dma(out_ap=T.land[:, W * r:W * r + W], in_ap=T.gat[:, W * q:W * q + W], remote_sem=T.sem["ar%d" % r],
+                         local_sem=T.sem.ls, pid=pid, routing_id=rid, dma_engine_mask=_mk(lo))
+            sent[0] += len(lo)
+        else:
+            k = cross.index(q)
+            rid, pid = topo.addr(relays[k % 2], core)
+            g.remote_dma(out_ap=T.rt[:, W * (k // 2):W * (k // 2) + W], in_ap=T.gat[:, W * q:W * q + W],
+                         remote_sem=T.sem["rt%d" % (k // 2)], local_sem=T.sem.ls, pid=pid, routing_id=rid,
+                         dma_engine_mask=_mk(hi))
+            sent[0] += len(hi)
+
+    order = [r] + same + cross
+    for k, q in enumerate(order):
+        gather(q)
+        if k >= 3:
+            send(order[k - 2])
+    send(order[-2])
+    send(order[-1])
+
+    d1, d2, d3, d4, d5, d6, d7, d8, d9, d10 = [sem() for k in range(10)]
+    V.tensor_scalar(T.ow256[:, :], T.owf[:, :], 256.0, None, A.mult).then_inc(d1, 1)
+    V.wait_ge(s_pidx, 1)
+    V.tensor_scalar(T.pci[:, 0:1], T.pidx[:, :], 1, 15, A.logical_shift_right, A.bitwise_and).then_inc(d2, 1)
+    V.tensor_scalar(T.pci[:, 1:2], T.pidx[:, :], 1, None, A.bitwise_and).then_inc(d2, 1)
+    V.tensor_scalar(T.pci[:, 2:3], T.pidx[:, :], 5, None, A.logical_shift_right).then_inc(d2, 1)
+    V.wait_ge(d1, 1)
+    V.tensor_tensor(T.slot[:, :], T.ow256[:, :], T.pos[:, :], A.add).then_inc(d3, 1)
+    V.wait_ge(d2, 3)
+    V.tensor_copy(T.pcf[:, :], T.pci[:, :]).then_inc(d4, 1)
+    V.wait_ge(d4, 1)
+    V.tensor_scalar(T.kcol[:, :], T.pcf[:, 1:2], 8.0, T.pcf[:, 2:3], A.mult, A.add).then_inc(d5, 1)
+    V.wait_ge(s_rowm, 1)
+    V.tensor_scalar(T.emat[:, :], T.rowm[:, :], T.pcf[:, 0:1], None, A.is_equal).then_inc(d6, 1)
+    V.wait_ge(d5, 1)
+    V.wait_ge(s_vm, 1)
+    V.tensor_scalar(T.mmat[:, :], T.vmask[:, :], T.kcol[:, :], None, A.is_equal).then_inc(d7, 1)
+    V.wait_ge(d7, 1)
+    V.wait_ge(d3, 1)
+    for c in range(4):
+        V.tensor_scalar(T.orh[:, 32 * c:32 * c + 32], T.mmat[:, 32 * c:32 * c + 32], T.slot[:, c:c + 1], None,
+                        A.mult).then_inc(d8, 1)
+    TE.wait_ge(d8, 4)
+    TE.wait_ge(d6, 1)
+    for c in range(4):
+        TE.matmul(T.po[:, 0:32], T.emat[:, :], T.orh[:, 32 * c:32 * c + 32], c == 0, c == 3).then_inc(d9, 1)
+    V.wait_ge(d9, 4)
+    V.tensor_copy(T.off[:, :], T.po[:, 0:32]).then_inc(d10, 1)
+
+    pin = [T.pin0, T.pin1]
+    tr = [sem() for k in range(N)]
+    cp = [sem() for k in range(N)]
+    TE.wait_ge(s_id, 1)
+    for k, o in enumerate(order):
+        if o == r:
+            TE.wait_ge(T.sem["gs%d" % r], 16)
+        else:
+            TE.wait_ge(T.sem["ar%d" % o], len(lo))
+        if k >= 2:
+            TE.wait_ge(cp[k - 2], 1)
+        for h in range(2):
+            TE.transpose(pin[k % 2][:, 128 * h:128 * h + 128], T.land[:, W * o + 128 * h:W * o + 128 * h + 128],
+                         T.ident[:, :]).then_inc(tr[k], 1)
+        V.wait_ge(tr[k], 2)
+        V.tensor_copy(T.rtw[:, W * o:W * o + W], pin[k % 2][:, 0:W]).then_inc(cp[k], 1)
+
+    pout = [T.pout0, T.pout1]
+    yg, tb, yc, st = [sem(), sem()], [sem(), sem()], [sem(), sem()], [sem(), sem()]
+    for k in range(N):
+        V.wait_ge(cp[k], 1)
+    V.wait_ge(d10, 1)
+    span = (N - 1) * W + CAP
+    for H in range(2):
+        for h in range(2):
+            V.tensor_copy(T.yt[:, 512 * H + 256 * h:512 * H + 256 * h + 256],
+                          T.rtw[:, 128 * h:128 * h + span].indirect(T.off[:, 16 * H:16 * H + 16])).then_inc(yg[H], 1)
+    for H in range(2):
+        TE.wait_ge(yg[H], 2)
+        for e in range(2):
+            for h in range(2):
+                TE.transpose(pout[H][:, 256 * e + 128 * h:256 * e + 128 * h + 128],
+                             T.yt[:, 512 * H + 256 * h + 128 * e:512 * H + 256 * h + 128 * e + 128],
+                             T.ident[:, :]).then_inc(tb[H], 1)
+        V.wait_ge(tb[H], 4)
+        V.tensor_copy(T.ysb[:, 512 * H:512 * H + 512], pout[H][:, 0:512]).then_inc(yc[H], 1)
+        Q = SY if H == 0 else SC
+        Q.wait_ge(yc[H], 1)
+        Q.dma_start(T.y[256 * H:256 * H + 256, :], T.ysb[:, 512 * H:512 * H + 512]).then_inc(st[H], 16)
+        Q.wait_ge(st[H], 16)
+
+    g.wait_ge(T.sem.ls, sent[0])

@@ -8,6 +8,7 @@ N = 8
 W = 256
 CAP = 128
 NPOOL = 64
+A = AluOpType
 
 SCRATCH = {
     "ix": ("sbuf", [128, 4], "int32"),
@@ -36,8 +37,7 @@ SCRATCH = {
     "kcol": ("sbuf", [128, 1], "float32"),
     "rowm": ("sbuf", [128, 128], "float32"),
     "vmask": ("sbuf", [128, 128], "float32"),
-    "emat": ("sbuf", [128, 128], "float32"),
-    "mmat": ("sbuf", [128, 128], "float32"),
+    "em": ("sbuf", [128, 256], "float32"),
     "orh": ("sbuf", [128, 128], "float32"),
     "off": ("sbuf", [128, 32], "uint16"),
     "gat": ("sbuf", [128, N * W], "bfloat16"),
@@ -45,7 +45,6 @@ SCRATCH = {
     "rtw": ("sbuf", [128, N * W], "bfloat16"),
     "yt": ("sbuf", [128, 1024], "bfloat16"),
     "ysb": ("sbuf", [128, 1024], "bfloat16"),
-    "rl": ("sbuf", [128, 8], "int32"),
     "rt": ("sbuf", [128, 2 * W], "bfloat16"),
     "pc": ("psum", [128, 512], "float32"),
     "pl": ("psum", [128, 512], "float32"),
@@ -56,7 +55,7 @@ SCRATCH = {
     "pout1": ("psum", [128, 1024], "bfloat16"),
 }
 SEMAPHORES = (["c%d" % k for k in range(NPOOL)] + ["rs%d" % k for k in range(N)] + ["ar%d" % k for k in range(N)]
-              + ["gs%d" % k for k in range(N)] + ["rq", "rt0", "rt1", "ls"])
+              + ["gs%d" % k for k in range(N)] + ["rq", "rt0", "rt1", "ls", "k0", "k1"])
 
 
 def _bits(mask):
@@ -81,24 +80,127 @@ def _split_direct(lo):
     return [lo[0:h], lo[h:h + q], lo[h + q:h + 2 * q]]
 
 
+def _pool(T):
+    cnt = [0]
+
+    def sem():
+        cnt[0] += 1
+        return T.sem["c%d" % (cnt[0] - 1)]
+    return sem
+
+
+def _consts(g, T, sem):
+    V = g.vector
+    cs = {k: sem() for k in ("ones", "z", "io8", "up", "io128")}
+    V.memset(T.ones[:, :], 1.0).then_inc(cs["ones"], 1)
+    V.memset(T.ohz[:, 0:24], 0.0).then_inc(cs["z"], 1)
+    g.iota(T.io8[:, :], [[1, 8]], 0, 0, allow_small_or_imprecise_dtypes=True).then_inc(cs["io8"], 1)
+    g.wait_ge(cs["ones"], 1)
+    g.affine_select(T.upper[:, :], T.ones[:, :], [[1, 128]], A.is_ge, 0.0, -1, -1).then_inc(cs["up"], 1)
+    g.iota(T.io128[:, :], [[1, 128]], 0, 0, allow_small_or_imprecise_dtypes=True).then_inc(cs["io128"], 1)
+    return cs
+
+
+def _lists(g, T, sem, cs, s_ix, n_ix):
+    V, TE, SC = g.vector, g.tensor, g.scalar
+    a1, a2, a3, a4, a5, a6, a7, a8 = sem(), sem(), sem(), sem(), sem(), sem(), sem(), sem()
+    b1, b2, a10, a11 = sem(), sem(), sem(), sem()
+    a9 = [sem() for c in range(4)]
+    V.wait_ge(s_ix, n_ix)
+    V.tensor_scalar(T.owi[:, :], T.ix[:, :], 12, None, A.logical_shift_right).then_inc(a1, 1)
+    V.tensor_scalar(T.lci[:, 0:4], T.ix[:, :], 4032, None, A.bitwise_and).then_inc(a3, 1)
+    V.tensor_scalar(T.lci[:, 4:8], T.ix[:, :], 63, None, A.bitwise_and).then_inc(a3, 1)
+    V.wait_ge(a1, 1)
+    V.tensor_copy(T.owf[:, :], T.owi[:, :]).then_inc(a2, 1)
+    V.wait_ge(a2, 1)
+    V.wait_ge(cs["io8"], 1)
+    for c in range(4):
+        V.tensor_scalar(T.ohz[:, 24 + 8 * c:32 + 8 * c], T.io8[:, :], T.owf[:, c:c + 1], None, A.is_equal).then_inc(a4, 1)
+    V.wait_ge(a3, 2)
+    V.tensor_copy(T.lcf[:, :], T.lci[:, :]).then_inc(a5, 1)
+    TE.wait_ge(a4, 4)
+    TE.wait_ge(cs["z"], 1)
+    TE.wait_ge(cs["up"], 1)
+    TE.wait_ge(cs["ones"], 1)
+    TE.matmul(T.pc[:, 0:32], T.upper[:, :], T.ohz[:, 24:56], True, False).then_inc(b1, 1)
+    for k in range(1, 4):
+        TE.matmul(T.pc[:, 0:32], T.ones[:, :], T.ohz[:, 24 - 8 * k:56 - 8 * k], False, k == 3).then_inc(b1, 1)
+    SC.wait_ge(a4, 4)
+    SC.wait_ge(a5, 1)
+    for c in range(4):
+        for part in range(2):
+            SC.activation(T.rv[:, 16 * c + 8 * part:16 * c + 8 * part + 8], T.ohz[:, 24 + 8 * c:32 + 8 * c],
+                          ActivationFunctionType.Copy, scale=T.lcf[:, 4 * part + c:4 * part + c + 1]).then_inc(a6, 1)
+    V.wait_ge(b1, 4)
+    V.tensor_tensor(T.prod[:, :], T.ohz[:, 24:56], T.pc[:, 0:32], A.mult).then_inc(a7, 1)
+    V.wait_ge(a7, 1)
+    for c in range(4):
+        V.tensor_reduce(T.pos[:, c:c + 1], T.prod[:, 8 * c:8 * c + 8], AxisListType.X, A.add).then_inc(a8, 1)
+    V.wait_ge(a8, 4)
+    V.wait_ge(cs["io128"], 1)
+    for c in range(4):
+        V.tensor_scalar(T.pm[:, 128 * c:128 * c + 128], T.io128[:, :], T.pos[:, c:c + 1], None, A.is_equal).then_inc(a9[c], 1)
+    TE.wait_ge(a6, 8)
+    for c in range(4):
+        TE.wait_ge(a9[c], 1)
+        TE.matmul(T.pl[:, 0:16], T.pm[:, 128 * c:128 * c + 128], T.rv[:, 16 * c:16 * c + 16], c == 0, c == 3).then_inc(b2, 1)
+    V.wait_ge(b2, 4)
+    V.tensor_copy(T.la[:, :], T.pl[:, 0:8]).then_inc(a10, 1)
+    V.wait_ge(a10, 1)
+    V.tensor_tensor(T.req[:, :], T.la[:, :], T.pl[:, 8:16], A.add).then_inc(a11, 1)
+    return a11
+
+
 def _relay(g, core, T, topo, cores, r, cross, i):
+    V = g.vector
+    sem = _pool(T)
     peers = cross[i::2]
     lo = _bits(topo.mask(core, cores[peers[0]]))
     half = len(lo) // 2
-    hi_n = (len(_bits(topo.mask(cores[r], core))) - len(lo)) // 2
-    g.wait_ge(T.sem.rq, hi_n)
+    n_on = len(_bits(topo.mask(cores[r], core)))
+    rid, pid = topo.addr(cores[r], core)
+    cs = _consts(g, T, sem)
+    if i == 0:
+        s_id = sem()
+        g.affine_select(T.ident[:, :], T.ones[:, :], [[-1, 128]], A.is_equal, 0.0, 0, 1).then_inc(s_id, 1)
+        g.wait_ge(s_id, 1)
+        g.remote_dma(out_ap=T.ident[:, :], in_ap=T.ident[:, :], remote_sem=T.sem.k0, local_sem=T.sem.ls, pid=pid,
+                     routing_id=rid, dma_engine_mask=_mk(lo))
+    else:
+        s_pidx, s_rowm, s_vm, d2, d4, d5, d6 = [sem() for k in range(7)]
+        g.iota(T.pidx[:, :], [[1, 1]], 0, 1).then_inc(s_pidx, 1)
+        g.iota(T.rowm[:, :], [[0, 8], [1, 16]], 0, 0, allow_small_or_imprecise_dtypes=True).then_inc(s_rowm, 1)
+        g.iota(T.vmask[:, :], [[-16, 2], [-4, 2], [1, 32]], 0, 0, allow_small_or_imprecise_dtypes=True).then_inc(s_vm, 1)
+        V.wait_ge(s_pidx, 1)
+        V.tensor_scalar(T.pci[:, 0:1], T.pidx[:, :], 1, 15, A.logical_shift_right, A.bitwise_and).then_inc(d2, 1)
+        V.tensor_scalar(T.pci[:, 1:2], T.pidx[:, :], 1, None, A.bitwise_and).then_inc(d2, 1)
+        V.tensor_scalar(T.pci[:, 2:3], T.pidx[:, :], 5, None, A.logical_shift_right).then_inc(d2, 1)
+        V.wait_ge(d2, 3)
+        V.tensor_copy(T.pcf[:, :], T.pci[:, :]).then_inc(d4, 1)
+        V.wait_ge(d4, 1)
+        V.tensor_scalar(T.kcol[:, :], T.pcf[:, 1:2], 8.0, T.pcf[:, 2:3], A.mult, A.add).then_inc(d5, 1)
+        V.wait_ge(s_rowm, 1)
+        V.tensor_scalar(T.em[:, 0:128], T.rowm[:, :], T.pcf[:, 0:1], None, A.is_equal).then_inc(d6, 1)
+        V.wait_ge(d5, 1)
+        V.wait_ge(s_vm, 1)
+        V.tensor_scalar(T.em[:, 128:256], T.vmask[:, :], T.kcol[:, :], None, A.is_equal).then_inc(d6, 1)
+        g.wait_ge(d6, 2)
+        g.remote_dma(out_ap=T.em[:, :], in_ap=T.em[:, :], remote_sem=T.sem.k1, local_sem=T.sem.ls, pid=pid,
+                     routing_id=rid, dma_engine_mask=_mk(lo))
+    ready = _lists(g, T, sem, cs, T.sem.rq, n_on // 2)
+    g.wait_ge(ready, 1)
     trs = []
     for j, q in enumerate(peers):
         rid, pid = topo.addr(cores[q], core)
         trs.append(RemoteDMATransfer(dst_ids=[DstId(rid=rid, pnc=pid)], dma_engine_mask=_mk(lo[half * j:half * j + half]),
-                                     remote_sem=T.sem["rs%d" % r], src=T.rl[:, :], dst=T.reqland[:, 8 * r:8 * r + 8]))
+                                     remote_sem=T.sem["rs%d" % r], src=T.req[:, :], dst=T.reqland[:, 8 * r:8 * r + 8]))
     g.remote_dma_fused(trs, local_sem=T.sem.ls)
     for j, q in enumerate(peers):
         rid, pid = topo.addr(cores[q], core)
-        g.wait_ge(T.sem["rt%d" % j], 2 * hi_n)
+        g.wait_ge(T.sem["rt%d" % j], n_on)
         g.remote_dma(out_ap=T.land[:, W * r:W * r + W], in_ap=T.rt[:, W * j:W * j + W], remote_sem=T.sem["ar%d" % r],
                      local_sem=T.sem.ls, pid=pid, routing_id=rid, dma_engine_mask=_mk(lo))
-    g.wait_ge(T.sem.ls, 2 * half + 2 * len(lo))
+    g.wait_ge(T.sem.ls, len(lo) + 2 * half + 2 * len(lo))
 
 
 def rank_program(g, core, T, topo):
@@ -113,93 +215,32 @@ def rank_program(g, core, T, topo):
         return
 
     V, TE, SC, SY = g.vector, g.tensor, g.scalar, g.sync
-    A = AluOpType
-    cnt = [0]
-
-    def sem():
-        cnt[0] += 1
-        return T.sem["c%d" % (cnt[0] - 1)]
-
+    sem = _pool(T)
     same, cross, relays = _plan(topo, cores, r)
     lo = _bits(topo.mask(core, cores[same[0]]))
     hi = [b for b in _bits(topo.mask(core, relays[0])) if b not in lo]
-    hh = len(hi) // 2
 
-    s_ix, s_ones, s_z = sem(), sem(), sem()
+    s_ix = sem()
     SY.dma_start(T.ix[:, :], T.idx[:, :]).then_inc(s_ix, 16)
-    V.memset(T.ones[:, :], 1.0).then_inc(s_ones, 1)
-    V.memset(T.ohz[:, 0:24], 0.0).then_inc(s_z, 1)
-    s_io8, s_up, s_io128, s_id, s_pidx, s_rowm, s_vm = sem(), sem(), sem(), sem(), sem(), sem(), sem()
-    g.iota(T.io8[:, :], [[1, 8]], 0, 0, allow_small_or_imprecise_dtypes=True).then_inc(s_io8, 1)
-    g.wait_ge(s_ones, 1)
-    g.affine_select(T.upper[:, :], T.ones[:, :], [[1, 128]], A.is_ge, 0.0, -1, -1).then_inc(s_up, 1)
-    g.iota(T.io128[:, :], [[1, 128]], 0, 0, allow_small_or_imprecise_dtypes=True).then_inc(s_io128, 1)
-    g.affine_select(T.ident[:, :], T.ones[:, :], [[-1, 128]], A.is_equal, 0.0, 0, 1).then_inc(s_id, 1)
-    g.iota(T.pidx[:, :], [[1, 1]], 0, 1).then_inc(s_pidx, 1)
-    g.iota(T.rowm[:, :], [[0, 8], [1, 16]], 0, 0, allow_small_or_imprecise_dtypes=True).then_inc(s_rowm, 1)
-    g.iota(T.vmask[:, :], [[-16, 2], [-4, 2], [1, 32]], 0, 0, allow_small_or_imprecise_dtypes=True).then_inc(s_vm, 1)
+    cs = _consts(g, T, sem)
+    g.wait_ge(s_ix, 16)
+    trs = []
+    for i, c in enumerate(relays):
+        rid, pid = topo.addr(c, core)
+        trs.append(RemoteDMATransfer(dst_ids=[DstId(rid=rid, pnc=pid)], dma_engine_mask=_mk([lo, hi][i]),
+                                     remote_sem=T.sem.rq, src=T.ix[:, :], dst=T.ix[:, :]))
+    g.remote_dma_fused(trs, local_sem=T.sem.ls)
+    sent = [len(lo) + len(hi)]
+    ready = _lists(g, T, sem, cs, s_ix, 16)
 
-    a1, a2, a3, a4, a5, a6, a7, a8 = sem(), sem(), sem(), sem(), sem(), sem(), sem(), sem()
-    b1, b2, a10, a11 = sem(), sem(), sem(), sem()
-    a9 = [sem() for c in range(4)]
-    V.wait_ge(s_ix, 16)
-    V.tensor_scalar(T.owi[:, :], T.ix[:, :], 12, None, A.logical_shift_right).then_inc(a1, 1)
-    V.tensor_scalar(T.lci[:, 0:4], T.ix[:, :], 4032, None, A.bitwise_and).then_inc(a3, 1)
-    V.tensor_scalar(T.lci[:, 4:8], T.ix[:, :], 63, None, A.bitwise_and).then_inc(a3, 1)
-    V.wait_ge(a1, 1)
-    V.tensor_copy(T.owf[:, :], T.owi[:, :]).then_inc(a2, 1)
-    V.wait_ge(a2, 1)
-    V.wait_ge(s_io8, 1)
-    for c in range(4):
-        V.tensor_scalar(T.ohz[:, 24 + 8 * c:32 + 8 * c], T.io8[:, :], T.owf[:, c:c + 1], None, A.is_equal).then_inc(a4, 1)
-    V.wait_ge(a3, 2)
-    V.tensor_copy(T.lcf[:, :], T.lci[:, :]).then_inc(a5, 1)
-
-    TE.wait_ge(a4, 4)
-    TE.wait_ge(s_z, 1)
-    TE.wait_ge(s_up, 1)
-    TE.wait_ge(s_ones, 1)
-    TE.matmul(T.pc[:, 0:32], T.upper[:, :], T.ohz[:, 24:56], True, False).then_inc(b1, 1)
-    for k in range(1, 4):
-        TE.matmul(T.pc[:, 0:32], T.ones[:, :], T.ohz[:, 24 - 8 * k:56 - 8 * k], False, k == 3).then_inc(b1, 1)
-
-    SC.wait_ge(a4, 4)
-    SC.wait_ge(a5, 1)
-    for c in range(4):
-        for part in range(2):
-            SC.activation(T.rv[:, 16 * c + 8 * part:16 * c + 8 * part + 8], T.ohz[:, 24 + 8 * c:32 + 8 * c],
-                          ActivationFunctionType.Copy, scale=T.lcf[:, 4 * part + c:4 * part + c + 1]).then_inc(a6, 1)
-
-    V.wait_ge(b1, 4)
-    V.tensor_tensor(T.prod[:, :], T.ohz[:, 24:56], T.pc[:, 0:32], A.mult).then_inc(a7, 1)
-    V.wait_ge(a7, 1)
-    for c in range(4):
-        V.tensor_reduce(T.pos[:, c:c + 1], T.prod[:, 8 * c:8 * c + 8], AxisListType.X, A.add).then_inc(a8, 1)
-    V.wait_ge(a8, 4)
-    V.wait_ge(s_io128, 1)
-    for c in range(4):
-        V.tensor_scalar(T.pm[:, 128 * c:128 * c + 128], T.io128[:, :], T.pos[:, c:c + 1], None, A.is_equal).then_inc(a9[c], 1)
-    TE.wait_ge(a6, 8)
-    for c in range(4):
-        TE.wait_ge(a9[c], 1)
-        TE.matmul(T.pl[:, 0:16], T.pm[:, 128 * c:128 * c + 128], T.rv[:, 16 * c:16 * c + 16], c == 0, c == 3).then_inc(b2, 1)
-    V.wait_ge(b2, 4)
-    V.tensor_copy(T.la[:, :], T.pl[:, 0:8]).then_inc(a10, 1)
-    V.wait_ge(a10, 1)
-    V.tensor_tensor(T.req[:, :], T.la[:, :], T.pl[:, 8:16], A.add).then_inc(a11, 1)
-
-    g.wait_ge(a11, 1)
+    g.wait_ge(ready, 1)
     trs = []
     for q, bl in zip(same, _split_direct(lo)):
         rid, pid = topo.addr(cores[q], core)
         trs.append(RemoteDMATransfer(dst_ids=[DstId(rid=rid, pnc=pid)], dma_engine_mask=_mk(bl),
                                      remote_sem=T.sem["rs%d" % r], src=T.req[:, :], dst=T.reqland[:, 8 * r:8 * r + 8]))
-    for i, c in enumerate(relays):
-        rid, pid = topo.addr(c, core)
-        trs.append(RemoteDMATransfer(dst_ids=[DstId(rid=rid, pnc=pid)], dma_engine_mask=_mk(hi[hh * i:hh * i + hh]),
-                                     remote_sem=T.sem.rq, src=T.req[:, :], dst=T.rl[:, :]))
+        sent[0] += len(bl)
     g.remote_dma_fused(trs, local_sem=T.sem.ls)
-    sent = [sum(len(bl) for bl in _split_direct(lo)) + 2 * hh]
 
     def req_count(q):
         qs, qc, qr = _plan(topo, cores, q)
@@ -219,59 +260,47 @@ def rank_program(g, core, T, topo):
     def send(q):
         g.wait_ge(T.sem["gs%d" % q], 16)
         if q in same:
-            rid, pid = topo.addr(cores[q], core)
-            g.remote_dma(out_ap=T.land[:, W * r:W * r + W], in_ap=T.gat[:, W * q:W * q + W], remote_sem=T.sem["ar%d" % r],
-                         local_sem=T.sem.ls, pid=pid, routing_id=rid, dma_engine_mask=_mk(lo))
-            sent[0] += len(lo)
+            bl, dcore = lo, cores[q]
+            dst, rsem = T.land[:, W * r:W * r + W], T.sem["ar%d" % r]
         else:
             k = cross.index(q)
-            rid, pid = topo.addr(relays[k % 2], core)
-            g.remote_dma(out_ap=T.rt[:, W * (k // 2):W * (k // 2) + W], in_ap=T.gat[:, W * q:W * q + W],
-                         remote_sem=T.sem["rt%d" % (k // 2)], local_sem=T.sem.ls, pid=pid, routing_id=rid,
-                         dma_engine_mask=_mk(hi))
-            sent[0] += len(hi)
+            bl, dcore = lo + hi, relays[k % 2]
+            dst, rsem = T.rt[:, W * (k // 2):W * (k // 2) + W], T.sem["rt%d" % (k // 2)]
+        rid, pid = topo.addr(dcore, core)
+        g.remote_dma(out_ap=dst, in_ap=T.gat[:, W * q:W * q + W], remote_sem=rsem, local_sem=T.sem.ls, pid=pid,
+                     routing_id=rid, dma_engine_mask=_mk(bl))
+        sent[0] += len(bl)
 
-    order = [r] + same + cross
-    for k, q in enumerate(order):
-        gather(q)
-        if k >= 3:
-            send(order[k - 2])
-    send(order[-2])
-    send(order[-1])
+    order = [r] + same[0:2] + cross + same[2:3]
+    gather(order[0])
+    gather(order[1])
+    for k in range(2, 7):
+        gather(order[k])
+        send(order[k - 1])
+    send(order[6])
+    gather(order[7])
+    send(order[7])
 
-    d1, d2, d3, d4, d5, d6, d7, d8, d9, d10 = [sem() for k in range(10)]
+    d1, d3, d8, d9, d10 = [sem() for k in range(5)]
     V.tensor_scalar(T.ow256[:, :], T.owf[:, :], 256.0, None, A.mult).then_inc(d1, 1)
-    V.wait_ge(s_pidx, 1)
-    V.tensor_scalar(T.pci[:, 0:1], T.pidx[:, :], 1, 15, A.logical_shift_right, A.bitwise_and).then_inc(d2, 1)
-    V.tensor_scalar(T.pci[:, 1:2], T.pidx[:, :], 1, None, A.bitwise_and).then_inc(d2, 1)
-    V.tensor_scalar(T.pci[:, 2:3], T.pidx[:, :], 5, None, A.logical_shift_right).then_inc(d2, 1)
     V.wait_ge(d1, 1)
     V.tensor_tensor(T.slot[:, :], T.ow256[:, :], T.pos[:, :], A.add).then_inc(d3, 1)
-    V.wait_ge(d2, 3)
-    V.tensor_copy(T.pcf[:, :], T.pci[:, :]).then_inc(d4, 1)
-    V.wait_ge(d4, 1)
-    V.tensor_scalar(T.kcol[:, :], T.pcf[:, 1:2], 8.0, T.pcf[:, 2:3], A.mult, A.add).then_inc(d5, 1)
-    V.wait_ge(s_rowm, 1)
-    V.tensor_scalar(T.emat[:, :], T.rowm[:, :], T.pcf[:, 0:1], None, A.is_equal).then_inc(d6, 1)
-    V.wait_ge(d5, 1)
-    V.wait_ge(s_vm, 1)
-    V.tensor_scalar(T.mmat[:, :], T.vmask[:, :], T.kcol[:, :], None, A.is_equal).then_inc(d7, 1)
-    V.wait_ge(d7, 1)
     V.wait_ge(d3, 1)
+    V.wait_ge(T.sem.k1, len(lo))
     for c in range(4):
-        V.tensor_scalar(T.orh[:, 32 * c:32 * c + 32], T.mmat[:, 32 * c:32 * c + 32], T.slot[:, c:c + 1], None,
+        V.tensor_scalar(T.orh[:, 32 * c:32 * c + 32], T.em[:, 128 + 32 * c:128 + 32 * c + 32], T.slot[:, c:c + 1], None,
                         A.mult).then_inc(d8, 1)
     TE.wait_ge(d8, 4)
-    TE.wait_ge(d6, 1)
+    TE.wait_ge(T.sem.k1, len(lo))
     for c in range(4):
-        TE.matmul(T.po[:, 0:32], T.emat[:, :], T.orh[:, 32 * c:32 * c + 32], c == 0, c == 3).then_inc(d9, 1)
+        TE.matmul(T.po[:, 0:32], T.em[:, 0:128], T.orh[:, 32 * c:32 * c + 32], c == 0, c == 3).then_inc(d9, 1)
     V.wait_ge(d9, 4)
     V.tensor_copy(T.off[:, :], T.po[:, 0:32]).then_inc(d10, 1)
 
     pin = [T.pin0, T.pin1]
     tr = [sem() for k in range(N)]
     cp = [sem() for k in range(N)]
-    TE.wait_ge(s_id, 1)
+    TE.wait_ge(T.sem.k0, len(lo))
     for k, o in enumerate(order):
         if o == r:
             TE.wait_ge(T.sem["gs%d" % r], 16)

@@ -1,35 +1,37 @@
 import numpy as np
 from concourse.bass import DstId, RemoteDMATransfer
-from concourse.bass import IndirectOffsetOnAxis
 from concourse.mybir import AluOpType, AxisListType, ActivationFunctionType
 
 NSIM = 256
 N = 8
 W = 256
 CAP = 128
-NPOOL = 64
+NPOOL = 110
 A = AluOpType
+COPY = ActivationFunctionType.Copy
 
 SCRATCH = {
     "ix": ("sbuf", [128, 4], "int32"),
     "owi": ("sbuf", [128, 4], "int32"),
-    "lci": ("sbuf", [128, 8], "int32"),
+    "lci": ("sbuf", [128, 12], "int32"),
     "owf": ("sbuf", [128, 4], "float32"),
-    "lcf": ("sbuf", [128, 8], "float32"),
-    "io8": ("sbuf", [128, 8], "float32"),
+    "lcf": ("sbuf", [128, 12], "float32"),
+    "lcm": ("sbuf", [128, 4], "float32"),
+    "lca": ("sbuf", [128, 4], "float32"),
     "ohz": ("sbuf", [128, 56], "bfloat16"),
     "ones": ("sbuf", [128, 128], "bfloat16"),
-    "upper": ("sbuf", [128, 128], "bfloat16"),
+    "cst": ("sbuf", [128, 352], "bfloat16"),
     "ident": ("sbuf", [128, 128], "bfloat16"),
-    "io128": ("sbuf", [128, 128], "bfloat16"),
-    "rv": ("sbuf", [128, 64], "bfloat16"),
+    "rv": ("sbuf", [128, 512], "bfloat16"),
     "prod": ("sbuf", [128, 32], "float32"),
-    "pos": ("sbuf", [128, 4], "float32"),
+    "key": ("sbuf", [128, 4], "float32"),
+    "keyi": ("sbuf", [128, 4], "int32"),
+    "kabi": ("sbuf", [128, 8], "int32"),
+    "kab": ("sbuf", [128, 8], "float32"),
     "pm": ("sbuf", [128, 512], "bfloat16"),
-    "la": ("sbuf", [128, 8], "float32"),
-    "req": ("sbuf", [128, 8], "int32"),
-    "reqland": ("sbuf", [128, 64], "int32"),
-    "ow256": ("sbuf", [128, 4], "float32"),
+    "reqoff": ("sbuf", [128, 64], "uint16"),
+    "offland": ("sbuf", [128, 64], "uint16"),
+    "ow128": ("sbuf", [128, 4], "float32"),
     "slot": ("sbuf", [128, 4], "float32"),
     "pidx": ("sbuf", [128, 1], "int32"),
     "pci": ("sbuf", [128, 3], "int32"),
@@ -40,22 +42,23 @@ SCRATCH = {
     "em": ("sbuf", [128, 256], "float32"),
     "orh": ("sbuf", [128, 128], "float32"),
     "off": ("sbuf", [128, 32], "uint16"),
+    "tabs": ("sbuf", [128, 8192], "bfloat16"),
+    "tabT": ("sbuf", [128, 8192], "bfloat16"),
     "gat": ("sbuf", [128, N * W], "bfloat16"),
     "land": ("sbuf", [128, N * W], "bfloat16"),
-    "rtw": ("sbuf", [128, N * W], "bfloat16"),
     "yt": ("sbuf", [128, 1024], "bfloat16"),
     "ysb": ("sbuf", [128, 1024], "bfloat16"),
     "rt": ("sbuf", [128, 2 * W], "bfloat16"),
     "pc": ("psum", [128, 512], "float32"),
     "pl": ("psum", [128, 512], "float32"),
     "po": ("psum", [128, 512], "float32"),
-    "pin0": ("psum", [128, 1024], "bfloat16"),
-    "pin1": ("psum", [128, 1024], "bfloat16"),
-    "pout0": ("psum", [128, 1024], "bfloat16"),
-    "pout1": ("psum", [128, 1024], "bfloat16"),
+    "pt0": ("psum", [128, 1024], "bfloat16"),
+    "pt1": ("psum", [128, 1024], "bfloat16"),
+    "pt2": ("psum", [128, 1024], "bfloat16"),
+    "pt3": ("psum", [128, 1024], "bfloat16"),
 }
 SEMAPHORES = (["c%d" % k for k in range(NPOOL)] + ["rs%d" % k for k in range(N)] + ["ar%d" % k for k in range(N)]
-              + ["gs%d" % k for k in range(N)] + ["rq", "rt0", "rt1", "ls", "k0", "k1"])
+              + ["rq", "rt0", "rt1", "ls", "lr", "k0", "k1", "k2"])
 
 
 def _bits(mask):
@@ -70,9 +73,11 @@ def _plan(topo, cores, r):
     me = cores[r]
     same = sorted([q for q in range(len(cores)) if q != r and topo.may_write(me, cores[q])], key=lambda q: q ^ r)
     cross = sorted([q for q in range(len(cores)) if q != r and q not in same], key=lambda q: q ^ r)
-    mates = [c for c in range(NSIM) if c != me and topo.host(c) == topo.host(me) and topo.chip(c) == topo.chip(me)]
-    relays = [c for c in mates if topo.die(c) == topo.die(me) and all(topo.may_write(c, cores[q]) for q in cross)][:2]
-    return same, cross, relays
+    mates = [c for c in range(NSIM) if c != me and topo.host(c) == topo.host(me) and topo.chip(c) == topo.chip(me)
+             and topo.die(c) == topo.die(me)]
+    relays = [c for c in mates if all(topo.may_write(c, cores[q]) for q in cross)][:2]
+    third = [c for c in mates if c not in relays and all(topo.may_write(c, cores[q]) for q in same)][0]
+    return same, cross, relays, third
 
 
 def _split_direct(lo):
@@ -89,118 +94,150 @@ def _pool(T):
     return sem
 
 
-def _consts(g, T, sem):
-    V = g.vector
-    cs = {k: sem() for k in ("ones", "z", "io8", "up", "io128")}
-    V.memset(T.ones[:, :], 1.0).then_inc(cs["ones"], 1)
-    V.memset(T.ohz[:, 0:24], 0.0).then_inc(cs["z"], 1)
-    g.iota(T.io8[:, :], [[1, 8]], 0, 0, allow_small_or_imprecise_dtypes=True).then_inc(cs["io8"], 1)
-    g.wait_ge(cs["ones"], 1)
-    g.affine_select(T.upper[:, :], T.ones[:, :], [[1, 128]], A.is_ge, 0.0, -1, -1).then_inc(cs["up"], 1)
-    g.iota(T.io128[:, :], [[1, 128]], 0, 0, allow_small_or_imprecise_dtypes=True).then_inc(cs["io128"], 1)
+def _fills(g, T, sem):
+    cs = {k: sem() for k in ("ones", "z")}
+    g.vector.memset(T.ones[:, :], 1.0).then_inc(cs["ones"], 1)
+    g.vector.memset(T.ohz[:, 0:24], 0.0).then_inc(cs["z"], 1)
     return cs
 
 
-def _lists(g, T, sem, cs, s_ix, n_ix):
-    V, TE, SC = g.vector, g.tensor, g.scalar
-    a1, a2, a3, a4, a5, a6, a7, a8 = sem(), sem(), sem(), sem(), sem(), sem(), sem(), sem()
-    b1, b2, a10, a11 = sem(), sem(), sem(), sem()
+def _consts(g, T, sem, cs):
+    s = sem()
+    g.iota(T.cst[:, 320:352], [[0, 4], [1, 8]], 0, 0, allow_small_or_imprecise_dtypes=True).then_inc(s, 1)
+    g.wait_ge(cs["ones"], 1)
+    g.affine_select(T.cst[:, 0:128], T.ones[:, :], [[1, 128]], A.is_ge, 0.0, -1, -1).then_inc(s, 1)
+    g.iota(T.cst[:, 128:256], [[0, 8], [1, 16]], 0, 0, allow_small_or_imprecise_dtypes=True).then_inc(s, 1)
+    g.iota(T.cst[:, 256:320], [[1, 64]], 0, 0, allow_small_or_imprecise_dtypes=True).then_inc(s, 1)
+    return s, 4
+
+
+def _lists(g, T, sem, cs, s_cst, n_cst, s_ix, n_ix, hooks=(None, None)):
+    V, TE = g.vector, g.tensor
+    a1, a2, a3, a4, a5, a6, a7, a8, a10, a11, a12, a13, a14, b1, b2 = [sem() for k in range(15)]
     a9 = [sem() for c in range(4)]
     V.wait_ge(s_ix, n_ix)
     V.tensor_scalar(T.owi[:, :], T.ix[:, :], 12, None, A.logical_shift_right).then_inc(a1, 1)
-    V.tensor_scalar(T.lci[:, 0:4], T.ix[:, :], 4032, None, A.bitwise_and).then_inc(a3, 1)
-    V.tensor_scalar(T.lci[:, 4:8], T.ix[:, :], 63, None, A.bitwise_and).then_inc(a3, 1)
+    V.tensor_scalar(T.lci[:, 0:4], T.ix[:, :], 3072, None, A.bitwise_and).then_inc(a3, 1)
+    V.tensor_scalar(T.lci[:, 4:8], T.ix[:, :], 7, None, A.bitwise_and).then_inc(a3, 1)
+    V.tensor_scalar(T.lci[:, 8:12], T.ix[:, :], 3, 127, A.logical_shift_right, A.bitwise_and).then_inc(a3, 1)
     V.wait_ge(a1, 1)
     V.tensor_copy(T.owf[:, :], T.owi[:, :]).then_inc(a2, 1)
     V.wait_ge(a2, 1)
-    V.wait_ge(cs["io8"], 1)
+    V.wait_ge(s_cst, n_cst)
     for c in range(4):
-        V.tensor_scalar(T.ohz[:, 24 + 8 * c:32 + 8 * c], T.io8[:, :], T.owf[:, c:c + 1], None, A.is_equal).then_inc(a4, 1)
-    V.wait_ge(a3, 2)
+        V.tensor_scalar(T.ohz[:, 24 + 8 * c:32 + 8 * c], T.cst[:, 320:328], T.owf[:, c:c + 1], None,
+                        A.is_equal).then_inc(a4, 1)
+    V.wait_ge(a3, 3)
     V.tensor_copy(T.lcf[:, :], T.lci[:, :]).then_inc(a5, 1)
+    V.wait_ge(a5, 1)
+    V.tensor_scalar(T.lcm[:, :], T.lcf[:, 4:8], 128.0, None, A.mult).then_inc(a6, 1)
+    V.wait_ge(a6, 1)
+    V.tensor_tensor(T.lca[:, :], T.lcf[:, 0:4], T.lcm[:, :], A.add).then_inc(a7, 1)
+    if hooks[0]:
+        hooks[0]()
     TE.wait_ge(a4, 4)
     TE.wait_ge(cs["z"], 1)
-    TE.wait_ge(cs["up"], 1)
+    TE.wait_ge(s_cst, n_cst)
     TE.wait_ge(cs["ones"], 1)
-    TE.matmul(T.pc[:, 0:32], T.upper[:, :], T.ohz[:, 24:56], True, False).then_inc(b1, 1)
+    TE.matmul(T.pc[:, 0:32], T.ones[:, :], T.cst[:, 320:352], True, False).then_inc(b1, 1)
+    TE.matmul(T.pc[:, 0:32], T.cst[:, 0:128], T.ohz[:, 24:56], False, False).then_inc(b1, 1)
     for k in range(1, 4):
         TE.matmul(T.pc[:, 0:32], T.ones[:, :], T.ohz[:, 24 - 8 * k:56 - 8 * k], False, k == 3).then_inc(b1, 1)
-    SC.wait_ge(a4, 4)
-    SC.wait_ge(a5, 1)
+    V.wait_ge(b1, 5)
+    V.tensor_tensor(T.prod[:, :], T.ohz[:, 24:56], T.pc[:, 0:32], A.mult).then_inc(a8, 1)
+    V.wait_ge(a8, 1)
     for c in range(4):
-        for part in range(2):
-            SC.activation(T.rv[:, 16 * c + 8 * part:16 * c + 8 * part + 8], T.ohz[:, 24 + 8 * c:32 + 8 * c],
-                          ActivationFunctionType.Copy, scale=T.lcf[:, 4 * part + c:4 * part + c + 1]).then_inc(a6, 1)
-    V.wait_ge(b1, 4)
-    V.tensor_tensor(T.prod[:, :], T.ohz[:, 24:56], T.pc[:, 0:32], A.mult).then_inc(a7, 1)
+        V.tensor_reduce(T.key[:, c:c + 1], T.prod[:, 8 * c:8 * c + 8], AxisListType.X, A.add).then_inc(a10, 1)
+    V.wait_ge(a10, 4)
+    V.tensor_copy(T.keyi[:, :], T.key[:, :]).then_inc(a12, 1)
+    V.wait_ge(a12, 1)
+    V.tensor_scalar(T.kabi[:, 0:4], T.keyi[:, :], 15, None, A.bitwise_and).then_inc(a13, 1)
+    V.tensor_scalar(T.kabi[:, 4:8], T.keyi[:, :], 4, None, A.logical_shift_right).then_inc(a13, 1)
+    V.wait_ge(a13, 2)
+    V.tensor_copy(T.kab[:, :], T.kabi[:, :]).then_inc(a14, 1)
+    V.wait_ge(a14, 1)
     V.wait_ge(a7, 1)
     for c in range(4):
-        V.tensor_reduce(T.pos[:, c:c + 1], T.prod[:, 8 * c:8 * c + 8], AxisListType.X, A.add).then_inc(a8, 1)
-    V.wait_ge(a8, 4)
-    V.wait_ge(cs["io128"], 1)
+        V.tensor_scalar(T.pm[:, 128 * c:128 * c + 128], T.cst[:, 128:256], T.kab[:, c:c + 1], None,
+                        A.is_equal).then_inc(a9[c], 1)
+        V.tensor_scalar(T.rv[:, 128 * c:128 * c + 64], T.cst[:, 256:320], T.kab[:, 4 + c:5 + c], T.lca[:, c:c + 1],
+                        A.is_equal, A.mult).then_inc(a9[c], 1)
+        V.tensor_scalar(T.rv[:, 128 * c + 64:128 * c + 128], T.cst[:, 256:320], T.kab[:, 4 + c:5 + c],
+                        T.lcf[:, 8 + c:9 + c], A.is_equal, A.mult).then_inc(a9[c], 1)
+    if hooks[1]:
+        hooks[1]()
     for c in range(4):
-        V.tensor_scalar(T.pm[:, 128 * c:128 * c + 128], T.io128[:, :], T.pos[:, c:c + 1], None, A.is_equal).then_inc(a9[c], 1)
-    TE.wait_ge(a6, 8)
-    for c in range(4):
-        TE.wait_ge(a9[c], 1)
-        TE.matmul(T.pl[:, 0:16], T.pm[:, 128 * c:128 * c + 128], T.rv[:, 16 * c:16 * c + 16], c == 0, c == 3).then_inc(b2, 1)
-    V.wait_ge(b2, 4)
-    V.tensor_copy(T.la[:, :], T.pl[:, 0:8]).then_inc(a10, 1)
-    V.wait_ge(a10, 1)
-    V.tensor_tensor(T.req[:, :], T.la[:, :], T.pl[:, 8:16], A.add).then_inc(a11, 1)
+        TE.wait_ge(a9[c], 3)
+        for part in range(2):
+            TE.matmul(T.pl[:, 0:64], T.pm[:, 128 * c:128 * c + 128], T.rv[:, 128 * c + 64 * part:128 * c + 64 * part + 64],
+                      c == 0 and part == 0, c == 3 and part == 1).then_inc(b2, 1)
+    V.wait_ge(b2, 8)
+    V.tensor_copy(T.reqoff[:, :], T.pl[:, 0:64]).then_inc(a11, 1)
     return a11
 
 
-def _relay(g, core, T, topo, cores, r, cross, i):
+def _helper(g, core, T, topo, cores, r, peers, masks, i, n_ix):
     V = g.vector
     sem = _pool(T)
-    peers = cross[i::2]
     lo = _bits(topo.mask(core, cores[peers[0]]))
-    half = len(lo) // 2
     n_on = len(_bits(topo.mask(cores[r], core)))
     rid, pid = topo.addr(cores[r], core)
-    cs = _consts(g, T, sem)
-    if i == 0:
-        s_id = sem()
-        g.affine_select(T.ident[:, :], T.ones[:, :], [[-1, 128]], A.is_equal, 0.0, 0, 1).then_inc(s_id, 1)
-        g.wait_ge(s_id, 1)
-        g.remote_dma(out_ap=T.ident[:, :], in_ap=T.ident[:, :], remote_sem=T.sem.k0, local_sem=T.sem.ls, pid=pid,
+    cs = _fills(g, T, sem)
+    s_cst, n_cst = _consts(g, T, sem, cs)
+    if i == 2:
+        g.wait_ge(s_cst, n_cst)
+        g.remote_dma(out_ap=T.cst[:, :], in_ap=T.cst[:, :], remote_sem=T.sem.k2, local_sem=T.sem.ls, pid=pid,
                      routing_id=rid, dma_engine_mask=_mk(lo))
     else:
-        s_pidx, s_rowm, s_vm, d2, d4, d5, d6 = [sem() for k in range(7)]
+        s_pidx, s_m, d2, d4, d5, d6 = [sem() for k in range(6)]
         g.iota(T.pidx[:, :], [[1, 1]], 0, 1).then_inc(s_pidx, 1)
-        g.iota(T.rowm[:, :], [[0, 8], [1, 16]], 0, 0, allow_small_or_imprecise_dtypes=True).then_inc(s_rowm, 1)
-        g.iota(T.vmask[:, :], [[-16, 2], [-4, 2], [1, 32]], 0, 0, allow_small_or_imprecise_dtypes=True).then_inc(s_vm, 1)
         V.wait_ge(s_pidx, 1)
-        V.tensor_scalar(T.pci[:, 0:1], T.pidx[:, :], 1, 15, A.logical_shift_right, A.bitwise_and).then_inc(d2, 1)
-        V.tensor_scalar(T.pci[:, 1:2], T.pidx[:, :], 1, None, A.bitwise_and).then_inc(d2, 1)
-        V.tensor_scalar(T.pci[:, 2:3], T.pidx[:, :], 5, None, A.logical_shift_right).then_inc(d2, 1)
-        V.wait_ge(d2, 3)
-        V.tensor_copy(T.pcf[:, :], T.pci[:, :]).then_inc(d4, 1)
-        V.wait_ge(d4, 1)
-        V.tensor_scalar(T.kcol[:, :], T.pcf[:, 1:2], 8.0, T.pcf[:, 2:3], A.mult, A.add).then_inc(d5, 1)
-        V.wait_ge(s_rowm, 1)
-        V.tensor_scalar(T.em[:, 0:128], T.rowm[:, :], T.pcf[:, 0:1], None, A.is_equal).then_inc(d6, 1)
-        V.wait_ge(d5, 1)
-        V.wait_ge(s_vm, 1)
-        V.tensor_scalar(T.em[:, 128:256], T.vmask[:, :], T.kcol[:, :], None, A.is_equal).then_inc(d6, 1)
-        g.wait_ge(d6, 2)
-        g.remote_dma(out_ap=T.em[:, :], in_ap=T.em[:, :], remote_sem=T.sem.k1, local_sem=T.sem.ls, pid=pid,
-                     routing_id=rid, dma_engine_mask=_mk(lo))
-    ready = _lists(g, T, sem, cs, T.sem.rq, n_on // 2)
+        if i == 0:
+            g.iota(T.rowm[:, :], [[0, 8], [1, 16]], 0, 0, allow_small_or_imprecise_dtypes=True).then_inc(s_m, 1)
+            V.tensor_scalar(T.pci[:, 0:1], T.pidx[:, :], 1, 15, A.logical_shift_right, A.bitwise_and).then_inc(d2, 1)
+            V.wait_ge(d2, 1)
+            V.tensor_copy(T.pcf[:, 0:1], T.pci[:, 0:1]).then_inc(d4, 1)
+            V.wait_ge(d4, 1)
+            V.wait_ge(s_m, 1)
+            V.tensor_scalar(T.em[:, 0:128], T.rowm[:, :], T.pcf[:, 0:1], None, A.is_equal).then_inc(d6, 1)
+        else:
+            g.iota(T.vmask[:, :], [[-16, 2], [-4, 2], [1, 32]], 0, 0, allow_small_or_imprecise_dtypes=True).then_inc(s_m, 1)
+            V.tensor_scalar(T.pci[:, 1:2], T.pidx[:, :], 1, None, A.bitwise_and).then_inc(d2, 1)
+            V.tensor_scalar(T.pci[:, 2:3], T.pidx[:, :], 5, None, A.logical_shift_right).then_inc(d2, 1)
+            V.wait_ge(d2, 2)
+            V.tensor_copy(T.pcf[:, 1:3], T.pci[:, 1:3]).then_inc(d4, 1)
+            V.wait_ge(d4, 1)
+            V.tensor_scalar(T.kcol[:, :], T.pcf[:, 1:2], 8.0, T.pcf[:, 2:3], A.mult, A.add).then_inc(d5, 1)
+            V.wait_ge(d5, 1)
+            V.wait_ge(s_m, 1)
+            V.tensor_scalar(T.em[:, 128:256], T.vmask[:, :], T.kcol[:, :], None, A.is_equal).then_inc(d6, 1)
+        g.wait_ge(d6, 1)
+        g.remote_dma(out_ap=T.em[:, 128 * i:128 * i + 128], in_ap=T.em[:, 128 * i:128 * i + 128],
+                     remote_sem=T.sem["k%d" % i], local_sem=T.sem.ls, pid=pid, routing_id=rid, dma_engine_mask=_mk(lo))
+    total = len(lo)
+    ready = _lists(g, T, sem, cs, s_cst, n_cst, T.sem.rq, n_ix)
     g.wait_ge(ready, 1)
     trs = []
-    for j, q in enumerate(peers):
+    for q, bl in zip(peers, masks):
         rid, pid = topo.addr(cores[q], core)
-        trs.append(RemoteDMATransfer(dst_ids=[DstId(rid=rid, pnc=pid)], dma_engine_mask=_mk(lo[half * j:half * j + half]),
-                                     remote_sem=T.sem["rs%d" % r], src=T.req[:, :], dst=T.reqland[:, 8 * r:8 * r + 8]))
+        trs.append(RemoteDMATransfer(dst_ids=[DstId(rid=rid, pnc=pid)], dma_engine_mask=_mk(bl),
+                                     remote_sem=T.sem["rs%d" % r], src=T.reqoff[:, 8 * q:8 * q + 8],
+                                     dst=T.offland[:, 8 * r:8 * r + 8]))
+        total += len(bl)
     g.remote_dma_fused(trs, local_sem=T.sem.ls)
-    for j, q in enumerate(peers):
-        rid, pid = topo.addr(cores[q], core)
-        g.wait_ge(T.sem["rt%d" % j], n_on)
-        g.remote_dma(out_ap=T.land[:, W * r:W * r + W], in_ap=T.rt[:, W * j:W * j + W], remote_sem=T.sem["ar%d" % r],
-                     local_sem=T.sem.ls, pid=pid, routing_id=rid, dma_engine_mask=_mk(lo))
-    g.wait_ge(T.sem.ls, len(lo) + 2 * half + 2 * len(lo))
+    if i < 2:
+        for j, q in enumerate(peers):
+            rid, pid = topo.addr(cores[q], core)
+            g.wait_ge(T.sem["rt%d" % j], n_on)
+            g.remote_dma(out_ap=T.land[:, W * r:W * r + W], in_ap=T.rt[:, W * j:W * j + W], remote_sem=T.sem["ar%d" % r],
+                         local_sem=T.sem.ls, pid=pid, routing_id=rid, dma_engine_mask=_mk(lo))
+            total += len(lo)
+    g.wait_ge(T.sem.ls, total)
+
+
+def _raw_masks(lo, hi):
+    half = len(lo) // 2
+    return [lo[0:half], lo[half:2 * half], hi]
 
 
 def rank_program(g, core, T, topo):
@@ -209,56 +246,124 @@ def rank_program(g, core, T, topo):
     if r is None:
         for q, rc in enumerate(cores):
             if topo.host(rc) == topo.host(core) and topo.chip(rc) == topo.chip(core):
-                same, cross, relays = _plan(topo, cores, q)
-                if core in relays:
-                    _relay(g, core, T, topo, cores, q, cross, relays.index(core))
+                same, cross, relays, third = _plan(topo, cores, q)
+                hs = relays + [third]
+                if core in hs:
+                    i = hs.index(core)
+                    lo = _bits(topo.mask(rc, cores[same[0]]))
+                    hi = [b for b in _bits(topo.mask(rc, core)) if b not in lo]
+                    n_ix = len(_raw_masks(lo, hi)[i])
+                    if i < 2:
+                        peers = cross[i::2]
+                        mine = _bits(topo.mask(core, cores[peers[0]]))
+                        half = len(mine) // 2
+                        masks = [mine[0:half], mine[half:2 * half]]
+                    else:
+                        peers = same
+                        masks = _split_direct(_bits(topo.mask(core, cores[peers[0]])))
+                    _helper(g, core, T, topo, cores, q, peers, masks, i, n_ix)
         return
 
     V, TE, SC, SY = g.vector, g.tensor, g.scalar, g.sync
     sem = _pool(T)
-    same, cross, relays = _plan(topo, cores, r)
+    same, cross, relays, third = _plan(topo, cores, r)
     lo = _bits(topo.mask(core, cores[same[0]]))
     hi = [b for b in _bits(topo.mask(core, relays[0])) if b not in lo]
 
-    s_ix = sem()
+    s_ix, s_id = sem(), sem()
+    tl = [sem() for k in range(4)]
     SY.dma_start(T.ix[:, :], T.idx[:, :]).then_inc(s_ix, 16)
-    cs = _consts(g, T, sem)
+    SC.dma_start(T.tabs[:, 0:2048], T.tab[0:1024, :]).then_inc(tl[0], 16)
+    SY.dma_start(T.tabs[:, 2048:4096], T.tab[1024:2048, :]).then_inc(tl[1], 16)
+    SY.wait_ge(T.sem.lr, len(lo) + len(hi))
+    SY.dma_start(T.tabs[:, 4096:6144], T.tab[2048:3072, :]).then_inc(tl[2], 16)
+    SY.dma_start(T.tabs[:, 6144:8192], T.tab[3072:4096, :]).then_inc(tl[3], 16)
+
+    cs = _fills(g, T, sem)
+    g.wait_ge(cs["ones"], 1)
+    g.affine_select(T.ident[:, :], T.ones[:, :], [[-1, 128]], A.is_equal, 0.0, 0, 1).then_inc(s_id, 1)
     g.wait_ge(s_ix, 16)
     trs = []
-    for i, c in enumerate(relays):
+    for c, bl in zip(relays + [third], _raw_masks(lo, hi)):
         rid, pid = topo.addr(c, core)
-        trs.append(RemoteDMATransfer(dst_ids=[DstId(rid=rid, pnc=pid)], dma_engine_mask=_mk([lo, hi][i]),
-                                     remote_sem=T.sem.rq, src=T.ix[:, :], dst=T.ix[:, :]))
-    g.remote_dma_fused(trs, local_sem=T.sem.ls)
-    sent = [len(lo) + len(hi)]
-    ready = _lists(g, T, sem, cs, s_ix, 16)
-
-    g.wait_ge(ready, 1)
-    trs = []
-    for q, bl in zip(same, _split_direct(lo)):
-        rid, pid = topo.addr(cores[q], core)
         trs.append(RemoteDMATransfer(dst_ids=[DstId(rid=rid, pnc=pid)], dma_engine_mask=_mk(bl),
-                                     remote_sem=T.sem["rs%d" % r], src=T.req[:, :], dst=T.reqland[:, 8 * r:8 * r + 8]))
-        sent[0] += len(bl)
-    g.remote_dma_fused(trs, local_sem=T.sem.ls)
+                                     remote_sem=T.sem.rq, src=T.ix[:, :], dst=T.ix[:, :]))
+    g.remote_dma_fused(trs, local_sem=T.sem.lr)
+
+    pt = [T.pt0, T.pt1, T.pt2, T.pt3]
+    tp = [sem() for b in range(8)]
+    ev = [sem() for b in range(8)]
+
+    def bank(b):
+        k, h = b // 2, b % 2
+        if h == 0:
+            TE.wait_ge(tl[k], 16)
+        if b >= 4:
+            TE.wait_ge(ev[b - 4], 1)
+        for i in range(8):
+            TE.transpose(pt[b % 4][:, 128 * i:128 * i + 128],
+                         T.tabs[:, 2048 * k + 256 * i + 128 * h:2048 * k + 256 * i + 128 * h + 128],
+                         T.ident[:, :]).then_inc(tp[b], 1)
+        out = T.tabT[:, 4096 * h + 1024 * k:4096 * h + 1024 * k + 1024]
+        if b in (5, 7):
+            V.wait_ge(tp[b], 8)
+            V.tensor_copy(out, pt[b % 4][:, :]).then_inc(ev[b], 1)
+        else:
+            SC.wait_ge(tp[b], 8)
+            SC.activation(out, pt[b % 4][:, :], COPY).then_inc(ev[b], 1)
+
+    def first():
+        TE.wait_ge(s_id, 1)
+        for b in range(0, 4):
+            bank(b)
+
+    def second():
+        for b in range(4, 6):
+            bank(b)
+
+    ready = _lists(g, T, sem, cs, T.sem.k2, len(lo), s_ix, 16, hooks=(first, second))
+
+    d1, d3, d8, d9, d10 = [sem() for k in range(5)]
+    V.tensor_scalar(T.ow128[:, :], T.owf[:, :], 128.0, None, A.mult).then_inc(d1, 1)
+    V.wait_ge(d1, 1)
+    V.tensor_tensor(T.slot[:, :], T.ow128[:, :], T.key[:, :], A.add).then_inc(d3, 1)
+    V.wait_ge(d3, 1)
+    V.wait_ge(T.sem.k1, len(lo))
+    for c in range(4):
+        V.tensor_scalar(T.orh[:, 32 * c:32 * c + 32], T.em[:, 128 + 32 * c:128 + 32 * c + 32], T.slot[:, c:c + 1], None,
+                        A.mult).then_inc(d8, 1)
+    for b in range(6, 8):
+        bank(b)
+    TE.wait_ge(d8, 4)
+    TE.wait_ge(T.sem.k0, len(lo))
+    for c in range(4):
+        TE.matmul(T.po[:, 0:32], T.em[:, 0:128], T.orh[:, 32 * c:32 * c + 32], c == 0, c == 3).then_inc(d9, 1)
 
     def req_count(q):
-        qs, qc, qr = _plan(topo, cores, q)
+        qs, qc, qr, qt = _plan(topo, cores, q)
         if r in qs:
-            return len(_split_direct(_bits(topo.mask(cores[q], core)))[qs.index(r)])
+            return len(_split_direct(_bits(topo.mask(qt, core)))[qs.index(r)])
         return len(_bits(topo.mask(qr[0], core))) // 2
 
-    def gather(q):
+    pk = [sem() for q in range(N)]
+    sent = [0]
+    for b in range(8):
+        (V if b % 2 == 0 else SC).wait_ge(ev[b], 1)
+
+    def pick(q):
         if q == r:
-            tile, out = T.req[:, r:r + 1], T.land[:, W * r:W * r + W]
+            V.wait_ge(ready, 1)
+            SC.wait_ge(ready, 1)
+            offs, out = T.reqoff[:, 8 * r:8 * r + 8], T.land
         else:
-            g.wait_ge(T.sem["rs%d" % q], req_count(q))
-            tile, out = T.reqland[:, 8 * q + r:8 * q + r + 1], T.gat[:, W * q:W * q + W]
-        g.indirect_dma_start(out=out, out_offset=None, in_=T.tab[:], in_offset=IndirectOffsetOnAxis(ap=tile, axis=0),
-                             bounds_check=4095).then_inc(T.sem["gs%d" % q], 16)
+            V.wait_ge(T.sem["rs%d" % q], req_count(q))
+            SC.wait_ge(T.sem["rs%d" % q], req_count(q))
+            offs, out = T.offland[:, 8 * q:8 * q + 8], T.gat
+        V.tensor_copy(out[:, W * q:W * q + 128], T.tabT[:, 0:4096].indirect(offs)).then_inc(pk[q], 1)
+        SC.activation(out[:, W * q + 128:W * q + 256], T.tabT[:, 4096:8192].indirect(offs), COPY).then_inc(pk[q], 1)
 
     def send(q):
-        g.wait_ge(T.sem["gs%d" % q], 16)
+        g.wait_ge(pk[q], 2)
         if q in same:
             bl, dcore = lo, cores[q]
             dst, rsem = T.land[:, W * r:W * r + W], T.sem["ar%d" % r]
@@ -271,59 +376,29 @@ def rank_program(g, core, T, topo):
                      routing_id=rid, dma_engine_mask=_mk(bl))
         sent[0] += len(bl)
 
-    order = [r] + same[0:2] + cross + same[2:3]
-    gather(order[0])
-    gather(order[1])
-    for k in range(2, 7):
-        gather(order[k])
-        send(order[k - 1])
-    send(order[6])
-    gather(order[7])
-    send(order[7])
+    order = [cross[0], cross[1], same[0], cross[2], cross[3], same[1], same[2]]
+    for q in order:
+        pick(q)
+        send(q)
+    pick(r)
 
-    d1, d3, d8, d9, d10 = [sem() for k in range(5)]
-    V.tensor_scalar(T.ow256[:, :], T.owf[:, :], 256.0, None, A.mult).then_inc(d1, 1)
-    V.wait_ge(d1, 1)
-    V.tensor_tensor(T.slot[:, :], T.ow256[:, :], T.pos[:, :], A.add).then_inc(d3, 1)
-    V.wait_ge(d3, 1)
-    V.wait_ge(T.sem.k1, len(lo))
-    for c in range(4):
-        V.tensor_scalar(T.orh[:, 32 * c:32 * c + 32], T.em[:, 128 + 32 * c:128 + 32 * c + 32], T.slot[:, c:c + 1], None,
-                        A.mult).then_inc(d8, 1)
-    TE.wait_ge(d8, 4)
-    TE.wait_ge(T.sem.k1, len(lo))
-    for c in range(4):
-        TE.matmul(T.po[:, 0:32], T.em[:, 0:128], T.orh[:, 32 * c:32 * c + 32], c == 0, c == 3).then_inc(d9, 1)
     V.wait_ge(d9, 4)
     V.tensor_copy(T.off[:, :], T.po[:, 0:32]).then_inc(d10, 1)
-
-    pin = [T.pin0, T.pin1]
-    tr = [sem() for k in range(N)]
-    cp = [sem() for k in range(N)]
-    TE.wait_ge(T.sem.k0, len(lo))
-    for k, o in enumerate(order):
-        if o == r:
-            TE.wait_ge(T.sem["gs%d" % r], 16)
-        else:
-            TE.wait_ge(T.sem["ar%d" % o], len(lo))
-        if k >= 2:
-            TE.wait_ge(cp[k - 2], 1)
-        for h in range(2):
-            TE.transpose(pin[k % 2][:, 128 * h:128 * h + 128], T.land[:, W * o + 128 * h:W * o + 128 * h + 128],
-                         T.ident[:, :]).then_inc(tr[k], 1)
-        V.wait_ge(tr[k], 2)
-        V.tensor_copy(T.rtw[:, W * o:W * o + W], pin[k % 2][:, 0:W]).then_inc(cp[k], 1)
-
-    pout = [T.pout0, T.pout1]
+    pout = [T.pt0, T.pt1]
     yg, tb, yc, st = [sem(), sem()], [sem(), sem()], [sem(), sem()], [sem(), sem()]
-    for k in range(N):
-        V.wait_ge(cp[k], 1)
-    V.wait_ge(d10, 1)
+    for Q in (V, SC):
+        Q.wait_ge(d10, 1)
+        Q.wait_ge(pk[r], 2)
+        for o in order:
+            Q.wait_ge(T.sem["ar%d" % o], len(lo))
     span = (N - 1) * W + CAP
-    for H in range(2):
-        for h in range(2):
-            V.tensor_copy(T.yt[:, 512 * H + 256 * h:512 * H + 256 * h + 256],
-                          T.rtw[:, 128 * h:128 * h + span].indirect(T.off[:, 16 * H:16 * H + 16])).then_inc(yg[H], 1)
+    for h in range(2):
+        V.tensor_copy(T.yt[:, 256 * h:256 * h + 256],
+                      T.land[:, 128 * h:128 * h + span].indirect(T.off[:, 0:16])).then_inc(yg[0], 1)
+        SC.activation(T.yt[:, 512 + 256 * h:512 + 256 * h + 256],
+                      T.land[:, 128 * h:128 * h + span].indirect(T.off[:, 16:32]), COPY).then_inc(yg[1], 1)
+    TE.wait_ge(ev[4], 1)
+    TE.wait_ge(ev[5], 1)
     for H in range(2):
         TE.wait_ge(yg[H], 2)
         for e in range(2):

@@ -48,7 +48,7 @@ SCRATCH = {
     "land": ("sbuf", [128, N * W], "bfloat16"),
     "yt": ("sbuf", [128, 1024], "bfloat16"),
     "ysb": ("sbuf", [128, 1024], "bfloat16"),
-    "rt": ("sbuf", [128, 2 * W], "bfloat16"),
+    "rt": ("sbuf", [128, W], "bfloat16"),
     "pc": ("psum", [128, 512], "float32"),
     "pl": ("psum", [128, 512], "float32"),
     "po": ("psum", [128, 512], "float32"),
@@ -58,7 +58,7 @@ SCRATCH = {
     "pt3": ("psum", [128, 1024], "bfloat16"),
 }
 SEMAPHORES = (["c%d" % k for k in range(NPOOL)] + ["rs%d" % k for k in range(N)] + ["ar%d" % k for k in range(N)]
-              + ["rq", "rt0", "rt1", "ls", "lr", "k0", "k1", "k2"])
+              + ["rq", "rt0", "ls", "lr", "k0", "k1", "k2", "k3"])
 
 
 def _bits(mask):
@@ -73,16 +73,21 @@ def _plan(topo, cores, r):
     me = cores[r]
     same = sorted([q for q in range(len(cores)) if q != r and topo.may_write(me, cores[q])], key=lambda q: q ^ r)
     cross = sorted([q for q in range(len(cores)) if q != r and q not in same], key=lambda q: q ^ r)
-    mates = [c for c in range(NSIM) if c != me and topo.host(c) == topo.host(me) and topo.chip(c) == topo.chip(me)
-             and topo.die(c) == topo.die(me)]
-    relays = [c for c in mates if all(topo.may_write(c, cores[q]) for q in cross)][:2]
-    third = [c for c in mates if c not in relays and all(topo.may_write(c, cores[q]) for q in same)][0]
-    return same, cross, relays, third
+    mates = [c for c in range(NSIM) if c != me and topo.host(c) == topo.host(me) and topo.chip(c) == topo.chip(me)]
+    relays = [c for c in mates if all(topo.may_write(c, cores[q]) for q in cross + same)]
+    relays = sorted(relays, key=lambda c: (topo.die(c) != topo.die(me), c))[:len(cross)]
+    return same, cross, relays
 
 
-def _split_direct(lo):
-    h, q = len(lo) // 2, len(lo) // 4
-    return [lo[0:h], lo[h:h + q], lo[h + q:h + 2 * q]]
+def _req_plan(topo, cores, q):
+    same, cross, relays = _plan(topo, cores, q)
+    plan = []
+    for i, c in enumerate(relays):
+        peers = [cross[i]] + same[i:i + 1]
+        bl = _bits(topo.mask(c, cores[peers[0]]))
+        n = len(bl) // len(peers)
+        plan.append([(o, bl[n * j:n * j + n]) for j, o in enumerate(peers)])
+    return plan
 
 
 def _pool(T):
@@ -111,7 +116,7 @@ def _consts(g, T, sem, cs):
     return s, 4
 
 
-def _lists(g, T, sem, cs, s_cst, n_cst, s_ix, n_ix, hooks=(None, None)):
+def _lists(g, T, sem, cs, cw, s_ix, n_ix, hooks=(None, None)):
     V, TE = g.vector, g.tensor
     a1, a2, a3, a4, a5, a6, a7, a8, a10, a11, a12, a13, a14, b1, b2 = [sem() for k in range(15)]
     a9 = [sem() for c in range(4)]
@@ -123,7 +128,8 @@ def _lists(g, T, sem, cs, s_cst, n_cst, s_ix, n_ix, hooks=(None, None)):
     V.wait_ge(a1, 1)
     V.tensor_copy(T.owf[:, :], T.owi[:, :]).then_inc(a2, 1)
     V.wait_ge(a2, 1)
-    V.wait_ge(s_cst, n_cst)
+    for sc, nc in cw:
+        V.wait_ge(sc, nc)
     for c in range(4):
         V.tensor_scalar(T.ohz[:, 24 + 8 * c:32 + 8 * c], T.cst[:, 320:328], T.owf[:, c:c + 1], None,
                         A.is_equal).then_inc(a4, 1)
@@ -137,7 +143,8 @@ def _lists(g, T, sem, cs, s_cst, n_cst, s_ix, n_ix, hooks=(None, None)):
         hooks[0]()
     TE.wait_ge(a4, 4)
     TE.wait_ge(cs["z"], 1)
-    TE.wait_ge(s_cst, n_cst)
+    for sc, nc in cw:
+        TE.wait_ge(sc, nc)
     TE.wait_ge(cs["ones"], 1)
     TE.matmul(T.pc[:, 0:32], T.ones[:, :], T.cst[:, 320:352], True, False).then_inc(b1, 1)
     TE.matmul(T.pc[:, 0:32], T.cst[:, 0:128], T.ohz[:, 24:56], False, False).then_inc(b1, 1)
@@ -176,17 +183,18 @@ def _lists(g, T, sem, cs, s_cst, n_cst, s_ix, n_ix, hooks=(None, None)):
     return a11
 
 
-def _helper(g, core, T, topo, cores, r, peers, masks, i, n_ix):
+def _helper(g, core, T, topo, cores, r, jobs, i, n_ix):
     V = g.vector
     sem = _pool(T)
-    lo = _bits(topo.mask(core, cores[peers[0]]))
+    lo = _bits(topo.mask(core, cores[jobs[0][0]]))
     n_on = len(_bits(topo.mask(cores[r], core)))
     rid, pid = topo.addr(cores[r], core)
     cs = _fills(g, T, sem)
     s_cst, n_cst = _consts(g, T, sem, cs)
-    if i == 2:
+    if i >= 2:
+        a, b = [(0, 128), (128, 352)][i - 2]
         g.wait_ge(s_cst, n_cst)
-        g.remote_dma(out_ap=T.cst[:, :], in_ap=T.cst[:, :], remote_sem=T.sem.k2, local_sem=T.sem.ls, pid=pid,
+        g.remote_dma(out_ap=T.cst[:, a:b], in_ap=T.cst[:, a:b], remote_sem=T.sem["k%d" % i], local_sem=T.sem.ls, pid=pid,
                      routing_id=rid, dma_engine_mask=_mk(lo))
     else:
         s_pidx, s_m, d2, d4, d5, d6 = [sem() for k in range(6)]
@@ -215,29 +223,27 @@ def _helper(g, core, T, topo, cores, r, peers, masks, i, n_ix):
         g.remote_dma(out_ap=T.em[:, 128 * i:128 * i + 128], in_ap=T.em[:, 128 * i:128 * i + 128],
                      remote_sem=T.sem["k%d" % i], local_sem=T.sem.ls, pid=pid, routing_id=rid, dma_engine_mask=_mk(lo))
     total = len(lo)
-    ready = _lists(g, T, sem, cs, s_cst, n_cst, T.sem.rq, n_ix)
+    ready = _lists(g, T, sem, cs, [(s_cst, n_cst)], T.sem.rq, n_ix)
     g.wait_ge(ready, 1)
     trs = []
-    for q, bl in zip(peers, masks):
+    for q, bl in jobs:
         rid, pid = topo.addr(cores[q], core)
         trs.append(RemoteDMATransfer(dst_ids=[DstId(rid=rid, pnc=pid)], dma_engine_mask=_mk(bl),
                                      remote_sem=T.sem["rs%d" % r], src=T.reqoff[:, 8 * q:8 * q + 8],
                                      dst=T.offland[:, 8 * r:8 * r + 8]))
         total += len(bl)
     g.remote_dma_fused(trs, local_sem=T.sem.ls)
-    if i < 2:
-        for j, q in enumerate(peers):
-            rid, pid = topo.addr(cores[q], core)
-            g.wait_ge(T.sem["rt%d" % j], n_on)
-            g.remote_dma(out_ap=T.land[:, W * r:W * r + W], in_ap=T.rt[:, W * j:W * j + W], remote_sem=T.sem["ar%d" % r],
-                         local_sem=T.sem.ls, pid=pid, routing_id=rid, dma_engine_mask=_mk(lo))
-            total += len(lo)
+    rid, pid = topo.addr(cores[jobs[0][0]], core)
+    g.wait_ge(T.sem.rt0, n_on)
+    g.remote_dma(out_ap=T.land[:, W * r:W * r + W], in_ap=T.rt[:, :], remote_sem=T.sem["ar%d" % r],
+                 local_sem=T.sem.ls, pid=pid, routing_id=rid, dma_engine_mask=_mk(lo))
+    total += len(lo)
     g.wait_ge(T.sem.ls, total)
 
 
-def _raw_masks(lo, hi):
-    half = len(lo) // 2
-    return [lo[0:half], lo[half:2 * half], hi]
+def _raw_masks(al, n):
+    k = len(al) // n
+    return [al[k * i:k * i + k] for i in range(n)]
 
 
 def rank_program(g, core, T, topo):
@@ -246,27 +252,16 @@ def rank_program(g, core, T, topo):
     if r is None:
         for q, rc in enumerate(cores):
             if topo.host(rc) == topo.host(core) and topo.chip(rc) == topo.chip(core):
-                same, cross, relays, third = _plan(topo, cores, q)
-                hs = relays + [third]
-                if core in hs:
-                    i = hs.index(core)
-                    lo = _bits(topo.mask(rc, cores[same[0]]))
-                    hi = [b for b in _bits(topo.mask(rc, core)) if b not in lo]
-                    n_ix = len(_raw_masks(lo, hi)[i])
-                    if i < 2:
-                        peers = cross[i::2]
-                        mine = _bits(topo.mask(core, cores[peers[0]]))
-                        half = len(mine) // 2
-                        masks = [mine[0:half], mine[half:2 * half]]
-                    else:
-                        peers = same
-                        masks = _split_direct(_bits(topo.mask(core, cores[peers[0]])))
-                    _helper(g, core, T, topo, cores, q, peers, masks, i, n_ix)
+                same, cross, relays = _plan(topo, cores, q)
+                if core in relays:
+                    i = relays.index(core)
+                    n_ix = len(_raw_masks(_bits(topo.mask(rc, core)), len(relays))[i])
+                    _helper(g, core, T, topo, cores, q, _req_plan(topo, cores, q)[i], i, n_ix)
         return
 
     V, TE, SC, SY = g.vector, g.tensor, g.scalar, g.sync
     sem = _pool(T)
-    same, cross, relays, third = _plan(topo, cores, r)
+    same, cross, relays = _plan(topo, cores, r)
     lo = _bits(topo.mask(core, cores[same[0]]))
     hi = [b for b in _bits(topo.mask(core, relays[0])) if b not in lo]
 
@@ -284,7 +279,7 @@ def rank_program(g, core, T, topo):
     g.affine_select(T.ident[:, :], T.ones[:, :], [[-1, 128]], A.is_equal, 0.0, 0, 1).then_inc(s_id, 1)
     g.wait_ge(s_ix, 16)
     trs = []
-    for c, bl in zip(relays + [third], _raw_masks(lo, hi)):
+    for c, bl in zip(relays, _raw_masks(lo + hi, len(relays))):
         rid, pid = topo.addr(c, core)
         trs.append(RemoteDMATransfer(dst_ids=[DstId(rid=rid, pnc=pid)], dma_engine_mask=_mk(bl),
                                      remote_sem=T.sem.rq, src=T.ix[:, :], dst=T.ix[:, :]))
@@ -321,7 +316,7 @@ def rank_program(g, core, T, topo):
         for b in range(4, 6):
             bank(b)
 
-    ready = _lists(g, T, sem, cs, T.sem.k2, len(lo), s_ix, 16, hooks=(first, second))
+    ready = _lists(g, T, sem, cs, [(T.sem.k2, len(lo)), (T.sem.k3, len(lo))], s_ix, 16, hooks=(first, second))
 
     d1, d3, d8, d9, d10 = [sem() for k in range(5)]
     V.tensor_scalar(T.ow128[:, :], T.owf[:, :], 128.0, None, A.mult).then_inc(d1, 1)
@@ -340,10 +335,7 @@ def rank_program(g, core, T, topo):
         TE.matmul(T.po[:, 0:32], T.em[:, 0:128], T.orh[:, 32 * c:32 * c + 32], c == 0, c == 3).then_inc(d9, 1)
 
     def req_count(q):
-        qs, qc, qr, qt = _plan(topo, cores, q)
-        if r in qs:
-            return len(_split_direct(_bits(topo.mask(qt, core)))[qs.index(r)])
-        return len(_bits(topo.mask(qr[0], core))) // 2
+        return [len(bl) for jobs in _req_plan(topo, cores, q) for o, bl in jobs if o == r][0]
 
     pk = [sem() for q in range(N)]
     sent = [0]
@@ -368,15 +360,14 @@ def rank_program(g, core, T, topo):
             bl, dcore = lo, cores[q]
             dst, rsem = T.land[:, W * r:W * r + W], T.sem["ar%d" % r]
         else:
-            k = cross.index(q)
-            bl, dcore = lo + hi, relays[k % 2]
-            dst, rsem = T.rt[:, W * (k // 2):W * (k // 2) + W], T.sem["rt%d" % (k // 2)]
+            bl, dcore = lo + hi, relays[cross.index(q)]
+            dst, rsem = T.rt[:, :], T.sem.rt0
         rid, pid = topo.addr(dcore, core)
         g.remote_dma(out_ap=dst, in_ap=T.gat[:, W * q:W * q + W], remote_sem=rsem, local_sem=T.sem.ls, pid=pid,
                      routing_id=rid, dma_engine_mask=_mk(bl))
         sent[0] += len(bl)
 
-    order = [cross[0], cross[1], same[0], cross[2], cross[3], same[1], same[2]]
+    order = cross + same
     for q in order:
         pick(q)
         send(q)
@@ -385,27 +376,28 @@ def rank_program(g, core, T, topo):
     V.wait_ge(d9, 4)
     V.tensor_copy(T.off[:, :], T.po[:, 0:32]).then_inc(d10, 1)
     pout = [T.pt0, T.pt1]
-    yg, tb, yc, st = [sem(), sem()], [sem(), sem()], [sem(), sem()], [sem(), sem()]
+    tb, yc, st = [sem(), sem()], [sem(), sem()], [sem(), sem()]
+    yg = [[sem() for u in range(4)] for H in range(2)]
     for Q in (V, SC):
         Q.wait_ge(d10, 1)
         Q.wait_ge(pk[r], 2)
         for o in order:
             Q.wait_ge(T.sem["ar%d" % o], len(lo))
     span = (N - 1) * W + CAP
-    for h in range(2):
-        V.tensor_copy(T.yt[:, 256 * h:256 * h + 256],
-                      T.land[:, 128 * h:128 * h + span].indirect(T.off[:, 0:16])).then_inc(yg[0], 1)
-        SC.activation(T.yt[:, 512 + 256 * h:512 + 256 * h + 256],
-                      T.land[:, 128 * h:128 * h + span].indirect(T.off[:, 16:32]), COPY).then_inc(yg[1], 1)
     TE.wait_ge(ev[4], 1)
     TE.wait_ge(ev[5], 1)
+    for u in range(4):
+        e, h = u // 2, u % 2
+        for H in range(2):
+            dst = T.yt[:, 512 * H + 256 * h + 128 * e:512 * H + 256 * h + 128 * e + 128]
+            src = T.land[:, 128 * h:128 * h + span].indirect(T.off[:, 16 * H + 8 * e:16 * H + 8 * e + 8])
+            if H == 0:
+                V.tensor_copy(dst, src).then_inc(yg[H][u], 1)
+            else:
+                SC.activation(dst, src, COPY).then_inc(yg[H][u], 1)
+            TE.wait_ge(yg[H][u], 1)
+            TE.transpose(pout[H][:, 256 * e + 128 * h:256 * e + 128 * h + 128], dst, T.ident[:, :]).then_inc(tb[H], 1)
     for H in range(2):
-        TE.wait_ge(yg[H], 2)
-        for e in range(2):
-            for h in range(2):
-                TE.transpose(pout[H][:, 256 * e + 128 * h:256 * e + 128 * h + 128],
-                             T.yt[:, 512 * H + 256 * h + 128 * e:512 * H + 256 * h + 128 * e + 128],
-                             T.ident[:, :]).then_inc(tb[H], 1)
         V.wait_ge(tb[H], 4)
         V.tensor_copy(T.ysb[:, 512 * H:512 * H + 512], pout[H][:, 0:512]).then_inc(yc[H], 1)
         Q = SY if H == 0 else SC

import numpy as np
from concourse.bass import DstId, RemoteDMATransfer
from concourse.mybir import AluOpType, AxisListType, ActivationFunctionType

NSIM = 256
N = 8
W = 256
CAP = 128
NPOOL = 110
A = AluOpType
COPY = ActivationFunctionType.Copy

SCRATCH = {
    "ix": ("sbuf", [128, 4], "int32"),
    "owi": ("sbuf", [128, 4], "int32"),
    "lci": ("sbuf", [128, 12], "int32"),
    "owf": ("sbuf", [128, 4], "float32"),
    "lcf": ("sbuf", [128, 12], "float32"),
    "lcm": ("sbuf", [128, 4], "float32"),
    "lca": ("sbuf", [128, 4], "float32"),
    "ohz": ("sbuf", [128, 56], "bfloat16"),
    "ones": ("sbuf", [128, 128], "bfloat16"),
    "cst": ("sbuf", [128, 352], "bfloat16"),
    "ident": ("sbuf", [128, 128], "bfloat16"),
    "rv": ("sbuf", [128, 512], "bfloat16"),
    "prod": ("sbuf", [128, 32], "float32"),
    "key": ("sbuf", [128, 4], "float32"),
    "keyi": ("sbuf", [128, 4], "int32"),
    "kabi": ("sbuf", [128, 8], "int32"),
    "kab": ("sbuf", [128, 8], "float32"),
    "pm": ("sbuf", [128, 512], "bfloat16"),
    "reqoff": ("sbuf", [128, 64], "uint16"),
    "offland": ("sbuf", [128, 64], "uint16"),
    "ow128": ("sbuf", [128, 4], "float32"),
    "slot": ("sbuf", [128, 4], "float32"),
    "pidx": ("sbuf", [128, 1], "int32"),
    "pci": ("sbuf", [128, 3], "int32"),
    "pcf": ("sbuf", [128, 3], "float32"),
    "kcol": ("sbuf", [128, 1], "float32"),
    "rowm": ("sbuf", [128, 128], "float32"),
    "vmask": ("sbuf", [128, 128], "float32"),
    "em": ("sbuf", [128, 256], "float32"),
    "orh": ("sbuf", [128, 128], "float32"),
    "off": ("sbuf", [128, 32], "uint16"),
    "tabs": ("sbuf", [128, 8192], "bfloat16"),
    "tabT": ("sbuf", [128, 8192], "bfloat16"),
    "gat": ("sbuf", [128, N * W], "bfloat16"),
    "land": ("sbuf", [128, N * W], "bfloat16"),
    "yt": ("sbuf", [128, 1024], "bfloat16"),
    "ysb": ("sbuf", [128, 1024], "bfloat16"),
    "rt": ("sbuf", [128, W], "bfloat16"),
    "pc": ("psum", [128, 512], "float32"),
    "pl": ("psum", [128, 512], "float32"),
    "po": ("psum", [128, 512], "float32"),
    "pt0": ("psum", [128, 1024], "bfloat16"),
    "pt1": ("psum", [128, 1024], "bfloat16"),
    "pt2": ("psum", [128, 1024], "bfloat16"),
    "pt3": ("psum", [128, 1024], "bfloat16"),
}
SEMAPHORES = (["c%d" % k for k in range(NPOOL)] + ["rs%d" % k for k in range(N)] + ["ar%d" % k for k in range(N)]
              + ["rq", "rt0", "ls", "lr", "k0", "k1", "k2", "k3"])


def _bits(mask):
    return [b for b in range(16) if (mask >> b) & 1]


def _mk(bl):
    return int(sum(1 << b for b in bl))


def _plan(topo, cores, r):
    me = cores[r]
    same = sorted([q for q in range(len(cores)) if q != r and topo.may_write(me, cores[q])], key=lambda q: q ^ r)
    cross = sorted([q for q in range(len(cores)) if q != r and q not in same], key=lambda q: q ^ r)
    mates = [c for c in range(NSIM) if c != me and topo.host(c) == topo.host(me) and topo.chip(c) == topo.chip(me)]
    relays = [c for c in mates if all(topo.may_write(c, cores[q]) for q in cross + same)]
    relays = sorted(relays, key=lambda c: (topo.die(c) != topo.die(me), c))[:len(cross)]
    return same, cross, relays


def _req_plan(topo, cores, q):
    same, cross, relays = _plan(topo, cores, q)
    plan = []
    for i, c in enumerate(relays):
        peers = [cross[i]] + same[i:i + 1]
        bl = _bits(topo.mask(c, cores[peers[0]]))
        n = len(bl) // len(peers)
        plan.append([(o, bl[n * j:n * j + n]) for j, o in enumerate(peers)])
    return plan


def _pool(T):
    cnt = [0]

    def sem():
        cnt[0] += 1
        return T.sem["c%d" % (cnt[0] - 1)]
    return sem


def _fills(g, T, sem):
    cs = {k: sem() for k in ("ones", "z")}
    g.vector.memset(T.ones[:, :], 1.0).then_inc(cs["ones"], 1)
    g.vector.memset(T.ohz[:, 0:24], 0.0).then_inc(cs["z"], 1)
    return cs


def _consts(g, T, sem, cs):
    s = sem()
    g.iota(T.cst[:, 320:352], [[0, 4], [1, 8]], 0, 0, allow_small_or_imprecise_dtypes=True).then_inc(s, 1)
    g.wait_ge(cs["ones"], 1)
    g.affine_select(T.cst[:, 0:128], T.ones[:, :], [[1, 128]], A.is_ge, 0.0, -1, -1).then_inc(s, 1)
    g.iota(T.cst[:, 128:256], [[0, 8], [1, 16]], 0, 0, allow_small_or_imprecise_dtypes=True).then_inc(s, 1)
    g.iota(T.cst[:, 256:320], [[1, 64]], 0, 0, allow_small_or_imprecise_dtypes=True).then_inc(s, 1)
    return s, 4


def _lists(g, T, sem, cs, cw, s_ix, n_ix, hooks=(None, None)):
    V, TE = g.vector, g.tensor
    a1, a2, a3, a4, a5, a6, a7, a8, a10, a11, a12, a13, a14, b1, b2 = [sem() for k in range(15)]
    a9 = [sem() for c in range(4)]
    V.wait_ge(s_ix, n_ix)
    V.tensor_scalar(T.owi[:, :], T.ix[:, :], 12, None, A.logical_shift_right).then_inc(a1, 1)
    V.tensor_scalar(T.lci[:, 0:4], T.ix[:, :], 3072, None, A.bitwise_and).then_inc(a3, 1)
    V.tensor_scalar(T.lci[:, 4:8], T.ix[:, :], 7, None, A.bitwise_and).then_inc(a3, 1)
    V.tensor_scalar(T.lci[:, 8:12], T.ix[:, :], 3, 127, A.logical_shift_right, A.bitwise_and).then_inc(a3, 1)
    V.wait_ge(a1, 1)
    V.tensor_copy(T.owf[:, :], T.owi[:, :]).then_inc(a2, 1)
    V.wait_ge(a2, 1)
    for sc, nc in cw:
        V.wait_ge(sc, nc)
    for c in range(4):
        V.tensor_scalar(T.ohz[:, 24 + 8 * c:32 + 8 * c], T.cst[:, 320:328], T.owf[:, c:c + 1], None,
                        A.is_equal).then_inc(a4, 1)
    V.wait_ge(a3, 3)
    V.tensor_copy(T.lcf[:, :], T.lci[:, :]).then_inc(a5, 1)
    V.wait_ge(a5, 1)
    V.tensor_scalar(T.lcm[:, :], T.lcf[:, 4:8], 128.0, None, A.mult).then_inc(a6, 1)
    V.wait_ge(a6, 1)
    V.tensor_tensor(T.lca[:, :], T.lcf[:, 0:4], T.lcm[:, :], A.add).then_inc(a7, 1)
    if hooks[0]:
        hooks[0]()
    TE.wait_ge(a4, 4)
    TE.wait_ge(cs["z"], 1)
    for sc, nc in cw:
        TE.wait_ge(sc, nc)
    TE.wait_ge(cs["ones"], 1)
    TE.matmul(T.pc[:, 0:32], T.ones[:, :], T.cst[:, 320:352], True, False).then_inc(b1, 1)
    TE.matmul(T.pc[:, 0:32], T.cst[:, 0:128], T.ohz[:, 24:56], False, False).then_inc(b1, 1)
    for k in range(1, 4):
        TE.matmul(T.pc[:, 0:32], T.ones[:, :], T.ohz[:, 24 - 8 * k:56 - 8 * k], False, k == 3).then_inc(b1, 1)
    V.wait_ge(b1, 5)
    V.tensor_tensor(T.prod[:, :], T.ohz[:, 24:56], T.pc[:, 0:32], A.mult).then_inc(a8, 1)
    V.wait_ge(a8, 1)
    for c in range(4):
        V.tensor_reduce(T.key[:, c:c + 1], T.prod[:, 8 * c:8 * c + 8], AxisListType.X, A.add).then_inc(a10, 1)
    V.wait_ge(a10, 4)
    V.tensor_copy(T.keyi[:, :], T.key[:, :]).then_inc(a12, 1)
    V.wait_ge(a12, 1)
    V.tensor_scalar(T.kabi[:, 0:4], T.keyi[:, :], 15, None, A.bitwise_and).then_inc(a13, 1)
    V.tensor_scalar(T.kabi[:, 4:8], T.keyi[:, :], 4, None, A.logical_shift_right).then_inc(a13, 1)
    V.wait_ge(a13, 2)
    V.tensor_copy(T.kab[:, :], T.kabi[:, :]).then_inc(a14, 1)
    V.wait_ge(a14, 1)
    V.wait_ge(a7, 1)
    for c in range(4):
        V.tensor_scalar(T.pm[:, 128 * c:128 * c + 128], T.cst[:, 128:256], T.kab[:, c:c + 1], None,
                        A.is_equal).then_inc(a9[c], 1)
        V.tensor_scalar(T.rv[:, 128 * c:128 * c + 64], T.cst[:, 256:320], T.kab[:, 4 + c:5 + c], T.lca[:, c:c + 1],
                        A.is_equal, A.mult).then_inc(a9[c], 1)
        V.tensor_scalar(T.rv[:, 128 * c + 64:128 * c + 128], T.cst[:, 256:320], T.kab[:, 4 + c:5 + c],
                        T.lcf[:, 8 + c:9 + c], A.is_equal, A.mult).then_inc(a9[c], 1)
    if hooks[1]:
        hooks[1]()
    for c in range(4):
        TE.wait_ge(a9[c], 3)
        for part in range(2):
            TE.matmul(T.pl[:, 0:64], T.pm[:, 128 * c:128 * c + 128], T.rv[:, 128 * c + 64 * part:128 * c + 64 * part + 64],
                      c == 0 and part == 0, c == 3 and part == 1).then_inc(b2, 1)
    V.wait_ge(b2, 8)
    V.tensor_copy(T.reqoff[:, :], T.pl[:, 0:64]).then_inc(a11, 1)
    return a11


def _helper(g, core, T, topo, cores, r, jobs, i, n_ix):
    V = g.vector
    sem = _pool(T)
    lo = _bits(topo.mask(core, cores[jobs[0][0]]))
    n_on = len(_bits(topo.mask(cores[r], core)))
    rid, pid = topo.addr(cores[r], core)
    cs = _fills(g, T, sem)
    s_cst, n_cst = _consts(g, T, sem, cs)
    if i >= 2:
        a, b = [(0, 128), (128, 352)][i - 2]
        g.wait_ge(s_cst, n_cst)
        g.remote_dma(out_ap=T.cst[:, a:b], in_ap=T.cst[:, a:b], remote_sem=T.sem["k%d" % i], local_sem=T.sem.ls, pid=pid,
                     routing_id=rid, dma_engine_mask=_mk(lo))
    else:
        s_pidx, s_m, d2, d4, d5, d6 = [sem() for k in range(6)]
        g.iota(T.pidx[:, :], [[1, 1]], 0, 1).then_inc(s_pidx, 1)
        V.wait_ge(s_pidx, 1)
        if i == 0:
            g.iota(T.rowm[:, :], [[0, 8], [1, 16]], 0, 0, allow_small_or_imprecise_dtypes=True).then_inc(s_m, 1)
            V.tensor_scalar(T.pci[:, 0:1], T.pidx[:, :], 1, 15, A.logical_shift_right, A.bitwise_and).then_inc(d2, 1)
            V.wait_ge(d2, 1)
            V.tensor_copy(T.pcf[:, 0:1], T.pci[:, 0:1]).then_inc(d4, 1)
            V.wait_ge(d4, 1)
            V.wait_ge(s_m, 1)
            V.tensor_scalar(T.em[:, 0:128], T.rowm[:, :], T.pcf[:, 0:1], None, A.is_equal).then_inc(d6, 1)
        else:
            g.iota(T.vmask[:, :], [[-16, 2], [-4, 2], [1, 32]], 0, 0, allow_small_or_imprecise_dtypes=True).then_inc(s_m, 1)
            V.tensor_scalar(T.pci[:, 1:2], T.pidx[:, :], 1, None, A.bitwise_and).then_inc(d2, 1)
            V.tensor_scalar(T.pci[:, 2:3], T.pidx[:, :], 5, None, A.logical_shift_right).then_inc(d2, 1)
            V.wait_ge(d2, 2)
            V.tensor_copy(T.pcf[:, 1:3], T.pci[:, 1:3]).then_inc(d4, 1)
            V.wait_ge(d4, 1)
            V.tensor_scalar(T.kcol[:, :], T.pcf[:, 1:2], 8.0, T.pcf[:, 2:3], A.mult, A.add).then_inc(d5, 1)
            V.wait_ge(d5, 1)
            V.wait_ge(s_m, 1)
            V.tensor_scalar(T.em[:, 128:256], T.vmask[:, :], T.kcol[:, :], None, A.is_equal).then_inc(d6, 1)
        g.wait_ge(d6, 1)
        g.remote_dma(out_ap=T.em[:, 128 * i:128 * i + 128], in_ap=T.em[:, 128 * i:128 * i + 128],
                     remote_sem=T.sem["k%d" % i], local_sem=T.sem.ls, pid=pid, routing_id=rid, dma_engine_mask=_mk(lo))
    total = len(lo)
    ready = _lists(g, T, sem, cs, [(s_cst, n_cst)], T.sem.rq, n_ix)
    g.wait_ge(ready, 1)
    trs = []
    for q, bl in jobs:
        rid, pid = topo.addr(cores[q], core)
        trs.append(RemoteDMATransfer(dst_ids=[DstId(rid=rid, pnc=pid)], dma_engine_mask=_mk(bl),
                                     remote_sem=T.sem["rs%d" % r], src=T.reqoff[:, 8 * q:8 * q + 8],
                                     dst=T.offland[:, 8 * r:8 * r + 8]))
        total += len(bl)
    g.remote_dma_fused(trs, local_sem=T.sem.ls)
    rid, pid = topo.addr(cores[jobs[0][0]], core)
    g.wait_ge(T.sem.rt0, n_on)
    g.remote_dma(out_ap=T.land[:, W * r:W * r + W], in_ap=T.rt[:, :], remote_sem=T.sem["ar%d" % r],
                 local_sem=T.sem.ls, pid=pid, routing_id=rid, dma_engine_mask=_mk(lo))
    total += len(lo)
    g.wait_ge(T.sem.ls, total)


def _raw_masks(al, n):
    k = len(al) // n
    return [al[k * i:k * i + k] for i in range(n)]


def rank_program(g, core, T, topo):
    cores = [int(c) for c in T.cores]
    r = T.rank_of(core)
    if r is None:
        for q, rc in enumerate(cores):
            if topo.host(rc) == topo.host(core) and topo.chip(rc) == topo.chip(core):
                same, cross, relays = _plan(topo, cores, q)
                if core in relays:
                    i = relays.index(core)
                    n_ix = len(_raw_masks(_bits(topo.mask(rc, core)), len(relays))[i])
                    _helper(g, core, T, topo, cores, q, _req_plan(topo, cores, q)[i], i, n_ix)
        return

    V, TE, SC, SY = g.vector, g.tensor, g.scalar, g.sync
    sem = _pool(T)
    same, cross, relays = _plan(topo, cores, r)
    lo = _bits(topo.mask(core, cores[same[0]]))
    hi = [b for b in _bits(topo.mask(core, relays[0])) if b not in lo]

    s_ix, s_id = sem(), sem()
    tl = [sem() for k in range(4)]
    SY.dma_start(T.ix[:, :], T.idx[:, :]).then_inc(s_ix, 16)
    SC.dma_start(T.tabs[:, 0:2048], T.tab[0:1024, :]).then_inc(tl[0], 16)
    SY.dma_start(T.tabs[:, 2048:4096], T.tab[1024:2048, :]).then_inc(tl[1], 16)
    SY.wait_ge(T.sem.lr, len(lo) + len(hi))
    SY.dma_start(T.tabs[:, 4096:6144], T.tab[2048:3072, :]).then_inc(tl[2], 16)
    SY.dma_start(T.tabs[:, 6144:8192], T.tab[3072:4096, :]).then_inc(tl[3], 16)

    cs = _fills(g, T, sem)
    g.wait_ge(cs["ones"], 1)
    g.affine_select(T.ident[:, :], T.ones[:, :], [[-1, 128]], A.is_equal, 0.0, 0, 1).then_inc(s_id, 1)
    g.wait_ge(s_ix, 16)
    trs = []
    for c, bl in zip(relays, _raw_masks(lo + hi, len(relays))):
        rid, pid = topo.addr(c, core)
        trs.append(RemoteDMATransfer(dst_ids=[DstId(rid=rid, pnc=pid)], dma_engine_mask=_mk(bl),
                                     remote_sem=T.sem.rq, src=T.ix[:, :], dst=T.ix[:, :]))
    g.remote_dma_fused(trs, local_sem=T.sem.lr)

    pt = [T.pt0, T.pt1, T.pt2, T.pt3]
    tp = [sem() for b in range(8)]
    ev = [sem() for b in range(8)]

    def bank(b):
        k, h = b // 2, b % 2
        if h == 0:
            TE.wait_ge(tl[k], 16)
        if b >= 4:
            TE.wait_ge(ev[b - 4], 1)
        for i in range(8):
            TE.transpose(pt[b % 4][:, 128 * i:128 * i + 128],
                         T.tabs[:, 2048 * k + 256 * i + 128 * h:2048 * k + 256 * i + 128 * h + 128],
                         T.ident[:, :]).then_inc(tp[b], 1)
        out = T.tabT[:, 4096 * h + 1024 * k:4096 * h + 1024 * k + 1024]
        if b in (5, 7):
            V.wait_ge(tp[b], 8)
            V.tensor_copy(out, pt[b % 4][:, :]).then_inc(ev[b], 1)
        else:
            SC.wait_ge(tp[b], 8)
            SC.activation(out, pt[b % 4][:, :], COPY).then_inc(ev[b], 1)

    def first():
        TE.wait_ge(s_id, 1)
        for b in range(0, 4):
            bank(b)

    def second():
        for b in range(4, 6):
            bank(b)

    ready = _lists(g, T, sem, cs, [(T.sem.k2, len(lo)), (T.sem.k3, len(lo))], s_ix, 16, hooks=(first, second))

    d1, d3, d8, d9, d10 = [sem() for k in range(5)]
    V.tensor_scalar(T.ow128[:, :], T.owf[:, :], 128.0, None, A.mult).then_inc(d1, 1)
    V.wait_ge(d1, 1)
    V.tensor_tensor(T.slot[:, :], T.ow128[:, :], T.key[:, :], A.add).then_inc(d3, 1)
    V.wait_ge(d3, 1)
    V.wait_ge(T.sem.k1, len(lo))
    for c in range(4):
        V.tensor_scalar(T.orh[:, 32 * c:32 * c + 32], T.em[:, 128 + 32 * c:128 + 32 * c + 32], T.slot[:, c:c + 1], None,
                        A.mult).then_inc(d8, 1)
    for b in range(6, 8):
        bank(b)
    TE.wait_ge(d8, 4)
    TE.wait_ge(T.sem.k0, len(lo))
    for c in range(4):
        TE.matmul(T.po[:, 0:32], T.em[:, 0:128], T.orh[:, 32 * c:32 * c + 32], c == 0, c == 3).then_inc(d9, 1)

    def req_count(q):
        return [len(bl) for jobs in _req_plan(topo, cores, q) for o, bl in jobs if o == r][0]

    pk = [sem() for q in range(N)]
    sent = [0]
    for b in range(8):
        (V if b % 2 == 0 else SC).wait_ge(ev[b], 1)

    def pick(q):
        if q == r:
            V.wait_ge(ready, 1)
            SC.wait_ge(ready, 1)
            offs, out = T.reqoff[:, 8 * r:8 * r + 8], T.land
        else:
            V.wait_ge(T.sem["rs%d" % q], req_count(q))
            SC.wait_ge(T.sem["rs%d" % q], req_count(q))
            offs, out = T.offland[:, 8 * q:8 * q + 8], T.gat
        V.tensor_copy(out[:, W * q:W * q + 128], T.tabT[:, 0:4096].indirect(offs)).then_inc(pk[q], 1)
        SC.activation(out[:, W * q + 128:W * q + 256], T.tabT[:, 4096:8192].indirect(offs), COPY).then_inc(pk[q], 1)

    def send(q):
        g.wait_ge(pk[q], 2)
        if q in same:
            bl, dcore = lo, cores[q]
            dst, rsem = T.land[:, W * r:W * r + W], T.sem["ar%d" % r]
        else:
            bl, dcore = lo + hi, relays[cross.index(q)]
            dst, rsem = T.rt[:, :], T.sem.rt0
        rid, pid = topo.addr(dcore, core)
        g.remote_dma(out_ap=dst, in_ap=T.gat[:, W * q:W * q + W], remote_sem=rsem, local_sem=T.sem.ls, pid=pid,
                     routing_id=rid, dma_engine_mask=_mk(bl))
        sent[0] += len(bl)

    order = cross + same
    for q in order:
        pick(q)
        send(q)
    pick(r)

    V.wait_ge(d9, 4)
    V.tensor_copy(T.off[:, :], T.po[:, 0:32]).then_inc(d10, 1)
    pout = [T.pt0, T.pt1]
    tb, yc, st = [sem(), sem()], [sem(), sem()], [sem(), sem()]
    yg = [[sem() for u in range(4)] for H in range(2)]
    for Q in (V, SC):
        Q.wait_ge(d10, 1)
        Q.wait_ge(pk[r], 2)
        for o in order:
            Q.wait_ge(T.sem["ar%d" % o], len(lo))
    span = (N - 1) * W + CAP
    TE.wait_ge(ev[4], 1)
    TE.wait_ge(ev[5], 1)
    for u in range(4):
        e, h = u // 2, u % 2
        for H in range(2):
            dst = T.yt[:, 512 * H + 256 * h + 128 * e:512 * H + 256 * h + 128 * e + 128]
            src = T.land[:, 128 * h:128 * h + span].indirect(T.off[:, 16 * H + 8 * e:16 * H + 8 * e + 8])
            if H == 0:
                V.tensor_copy(dst, src).then_inc(yg[H][u], 1)
            else:
                SC.activation(dst, src, COPY).then_inc(yg[H][u], 1)
            TE.wait_ge(yg[H][u], 1)
            TE.transpose(pout[H][:, 256 * e + 128 * h:256 * e + 128 * h + 128], dst, T.ident[:, :]).then_inc(tb[H], 1)
    for H in range(2):
        V.wait_ge(tb[H], 4)
        V.tensor_copy(T.ysb[:, 512 * H:512 * H + 512], pout[H][:, 0:512]).then_inc(yc[H], 1)
        Q = SY if H == 0 else SC
        Q.wait_ge(yc[H], 1)
        Q.dma_start(T.y[256 * H:256 * H + 256, :], T.ysb[:, 512 * H:512 * H + 512]).then_inc(st[H], 16)
        Q.wait_ge(st[H], 16)

    g.wait_ge(T.sem.ls, sent[0])
